import numpy as np
import ml_dtypes


def mxq(x, axis, fmt="e4m3"):
    dtype, down = {"e4m3": (ml_dtypes.float8_e4m3fn, 7), "e5m2": (ml_dtypes.float8_e5m2, 14)}[fmt]
    v = np.moveaxis(np.asarray(x, np.float32).astype(ml_dtypes.bfloat16).astype(np.float64), axis, -1)
    blocks = v.reshape(v.shape[:-1] + (-1, 32))
    amax = np.abs(blocks).max(-1, keepdims=True)
    byte = np.maximum(np.where(amax > 0, np.frexp(amax)[1] - 1 + 127, 0) - down, 1)
    scale = np.exp2(byte - 127.0)
    codes = (blocks / scale).astype(np.float32).astype(dtype).astype(np.float64)
    return np.moveaxis((codes * scale).reshape(v.shape), -1, axis)


WIDE = False


def mx_kscale(k):
    if not WIDE:
        return np.ones(k)
    levels = np.array([10, -10, 5, -5, 0])
    if k % 512:
        return np.exp2(np.random.permutation(np.resize(levels, k // 32))).repeat(32)
    a = np.empty((k // 512, 16))
    for p in range(k // 512):
        a[p, :8] = np.random.permutation(np.resize(levels, 8))
        for g in range(8):
            far = levels[np.abs(levels - a[p, g]) >= 10]
            a[p, g + 8] = far[np.random.randint(len(far))]
    return np.exp2(a.ravel()).repeat(32)


def f64(x):
    return np.asarray(x).astype(np.float64)


def striped(idx):
    return np.tile(idx.reshape(-1, 16).T, (8, 1)).astype(np.uint16)


def unstriped(offs):
    return offs[:16].T.reshape(-1).astype(np.int64)


E2M1 = np.array([0.0, 0.5, 1.0, 1.5, 2.0, 3.0, 4.0, 6.0, -0.0, -0.5, -1.0, -1.5, -2.0, -3.0, -4.0, -6.0])


def pack_weight(w, fmt):
    k, n = w.shape
    w = f64(np.asarray(w, np.float32).astype(ml_dtypes.bfloat16)).reshape(k // 32, 32, n)
    amax = np.abs(w).max(1)
    if fmt == "e4m3":
        byte = np.frexp(amax)[1] - 1 + 127 - 7
    else:
        mant, ex = np.frexp(amax / 6.0)
        byte = np.where(mant > 0.5, ex, ex - 1) + 127
    byte = np.clip(np.where(amax > 0, byte, 1), 1, 254)
    scaled = (w * np.exp2(127.0 - byte)[:, None, :]).reshape(k, n).astype(np.float32)
    by_word = np.ascontiguousarray(scaled.reshape(k // 512, 128, 4, n).transpose(0, 1, 3, 2))
    if fmt == "e4m3":
        words = by_word.astype(ml_dtypes.float8_e4m3fn).view(np.uint8)
    else:
        c = by_word.astype(ml_dtypes.float4_e2m1fn).view(np.uint8) & 0xF
        words = (c[..., 0::2] | (c[..., 1::2] << 4)).reshape(k // 512, 128, 2 * n)
    return np.ascontiguousarray(words), np.ascontiguousarray(byte.astype(np.uint8).reshape(k // 512, 16, n))


def unpack_weight(words, scales, fmt):
    g, _, n = scales.shape
    words = np.ascontiguousarray(words).reshape(g, 128, n, -1)
    if fmt == "e4m3":
        vals = words.view(ml_dtypes.float8_e4m3fn).astype(np.float64)
    else:
        nib = np.empty((g, 128, n, 4), np.uint8)
        nib[..., 0::2] = words & 0xF
        nib[..., 1::2] = words >> 4
        vals = E2M1[nib]
    vals = vals * np.repeat(np.exp2(scales.astype(np.float64) - 127.0), 8, axis=1)[..., None]
    return vals.transpose(0, 1, 3, 2).reshape(g * 512, n)


def gelu(v):
    return 0.5 * v * (1.0 + np.tanh(np.sqrt(2.0 / np.pi) * (v + 0.044715 * v**3)))


K, H, T, S, P, T2 = 1536, 512, 2048, 1024, 1024, 2048

def setup_inputs():
    n = np.random.standard_normal
    s = mx_kscale(K)[:, None]
    u = mx_kscale(H)[:, None]
    d = {}
    d["tab_words"], d["tab_scales"] = pack_weight(n((K, T)) * s, "e4m3")
    d["offs"] = striped(np.random.permutation(T)[:S])
    d["w1"] = (n((K, H)) / K ** 0.5 / s).astype(np.float32)
    d["base"] = n((H, S)).astype(np.float32)
    d["gain"] = (np.exp(0.3 * n(H)) * u[:, 0]).astype(np.float32)
    d["wgs"] = np.exp(0.3 * n((128, S))).astype(np.float32)
    d["page0"] = (1.5 * n((H, T2)) * u).astype(np.float32)
    d["offs2"] = striped(np.random.permutation(T2)[:S])
    d["offs3"] = striped(np.random.permutation(T2)[:P])
    d["knee"] = (np.exp(0.4 * n(H)) / u[:, 0]).astype(np.float32)
    d["w4_words"], d["w4_scales"] = pack_weight(3.0 * n((H, H)) / H ** 0.5 / u / u.T, "e2m1")
    d["wgo"] = np.exp(0.3 * n((128, P))).astype(np.float32)
    d["page1"] = n((H, T2)).astype(np.float32)
    d["offs4"] = striped(np.random.permutation(T2)[:P])
    return d

def reference(tab_words, tab_scales, offs, w1, base, gain, wgs, page0, offs2, offs3, knee,
              w4_words, w4_scales, wgo, page1, offs4):
    v = unpack_weight(tab_words, tab_scales, "e4m3")[:, unstriped(offs)]
    h = ((mxq(f64(w1), 0, "e4m3").T @ v) + f64(base)) * f64(gain)[:, None]
    page = f64(page0).copy()
    page[:, unstriped(offs2)] = np.tile(f64(wgs), (H // 128, 1)) * h
    xr = page[:, unstriped(offs3)]
    x = xr / (1.0 + f64(knee)[:, None] * np.abs(xr))
    w4 = unpack_weight(w4_words, w4_scales, "e2m1")
    y = (w4.T @ mxq(x, 0, "e4m3")) * x
    out = f64(page1).copy()
    out[:, unstriped(offs4)] = np.tile(f64(wgo), (H // 128, 1)) * y
    return out

@@ -1,0 +1,356 @@
+from contextlib import ExitStack
+
+import concourse.mybir as mybir
+from concourse.masks import make_identity
+
+K, H, T, S = 1536, 512, 2048, 1024
+FLOPS = 2 * K * H * S + 2 * H * H * S
+
+F32 = mybir.dt.float32
+BF16 = mybir.dt.bfloat16
+I32 = mybir.dt.int32
+U32 = mybir.dt.uint32
+U16 = mybir.dt.uint16
+U8 = mybir.dt.uint8
+FP8X4 = mybir.dt.float8_e4m3fn_x4
+FP4X4 = mybir.dt.float4_e2m1fn_x4
+MULT = mybir.AluOpType.mult
+ADD = mybir.AluOpType.add
+ACT = mybir.ActivationFunctionType
+
+P = 128
+PASSES = K // 512
+BLOCKS = H // P
+HALF = 512
+FIRST = slice(0, 256)
+REST = slice(256, 1024)
+GROUPS = (slice(0, 256), slice(256, 512), slice(512, 1024))
+
+
+def entries(offsets, cols):
+    return offsets[:, cols.start // 16 : cols.stop // 16]
+
+
+def tile_list_patch_pulse_page_kernel(
+    tc, tab_words, tab_scales, offs, w1, base, gain, wgs, page0, offs2, offs3, knee,
+    w4_words, w4_scales, wgo, page1, offs4, out,
+):
+    nc = tc.nc
+    with ExitStack() as ctx:
+        lists = ctx.enter_context(tc.tile_pool(name="lists", bufs=1))
+        keep = ctx.enter_context(tc.tile_pool(name="keep", bufs=1))
+        arena = ctx.enter_context(tc.tile_pool(name="arena", bufs=1))
+        psum = ctx.enter_context(tc.psum_pool(name="psum", bufs=1))
+
+        bank = [psum.tile([P, 512], F32, name=f"bank{i}") for i in range(8)]
+        idx1 = lists.tile([P, S // 16], U16, name="idx1")
+        idx2 = lists.tile([P, S // 16], U16, name="idx2")
+        idx3 = lists.tile([P, S // 16], U16, name="idx3")
+        idx4 = lists.tile([P, S // 16], U16, name="idx4")
+
+        tab_w = [keep.tile([P, T], I32, name=f"tab_w{a}") for a in range(PASSES)]
+        tab_s = keep.tile([P, T], U8, name="tab_s")
+        v_w = [keep.tile([P, S], U32, name=f"v_w{a}", align_bytes=64) for a in range(PASSES)]
+        v_s = keep.tile([P, S], U8, name="v_s", align_bytes=64)
+        raw0 = [keep.tile([P, 4, P], F32, name=f"raw0_{a}") for a in range(PASSES)]
+        raw1 = [keep.tile([P, 4, P], F32, name=f"raw1_{a}") for a in range(PASSES)]
+        raw23 = [arena.tile([P, 4, 2 * P], F32, name=f"raw23_{a}", offset=6144 + 4096 * a) for a in range(PASSES)]
+        w1_c = [keep.tile([P, PASSES * P], U32, name=f"w1_c{b}", align_bytes=64) for b in range(BLOCKS)]
+        w1_s = [keep.tile([P, PASSES * P], U8, name=f"w1_s{b}", align_bytes=64) for b in range(BLOCKS)]
+        base_t = [keep.tile([P, S], F32, name=f"base{b}") for b in range(BLOCKS)]
+        wgs_t = keep.tile([P, S], F32, name="wgs_t")
+        wg = [keep.tile([P, S], F32, name=f"wg{b}") for b in range(BLOCKS)]
+        rbuf1 = keep.tile([P, S], F32, name="rbuf1")
+        ebuf = keep.tile([P, S], F32, name="ebuf")
+        x0 = keep.tile([P, S], F32, name="x0")
+        xr0 = keep.tile([P, S], F32, name="xr0")
+        xr1 = keep.tile([P, S], F32, name="xr1")
+        pg0 = [keep.tile([P, T], F32, name=f"pg0_{b}") for b in range(BLOCKS)]
+        pg1 = [keep.tile([P, T], F32, name=f"pg1_{b}") for b in range(BLOCKS)]
+        wgo_t = keep.tile([P, S], F32, name="wgo_t")
+        x_t = [keep.tile([P, 4 * (g.stop - g.start)], BF16, name=f"x_t{i}") for i, g in enumerate(GROUPS)]
+        x_g = [keep.tile([P, 4 * (g.stop - g.start)], BF16, name=f"x_g{i}", align_bytes=64) for i, g in enumerate(GROUPS)]
+        x_c = [keep.tile([P, g.stop - g.start], U32, name=f"x_c{i}", align_bytes=64) for i, g in enumerate(GROUPS)]
+        x_s = [keep.tile([P, g.stop - g.start], U8, name=f"x_s{i}", align_bytes=64) for i, g in enumerate(GROUPS)]
+        w4_w = keep.tile([P, 2 * H], U8, name="w4_w", align_bytes=64)
+        w4_s = keep.tile([P, H], U8, name="w4_s", align_bytes=64)
+        ident = keep.tile([P, P], F32, name="ident")
+        vec_rows = keep.tile([P, P], F32, name="vec_rows")
+        vec_cols = keep.tile([P, 2 * BLOCKS], F32, name="vec_cols")
+        w1_b = [
+            keep.tile([P, PASSES * 512], BF16, name="w1_b0", align_bytes=64),
+            arena.tile([P, PASSES * 512], BF16, name="w1_b1", align_bytes=64, offset=0),
+            arena.tile([P, PASSES * 512], BF16, name="w1_b2", align_bytes=64, offset=3072),
+            keep.tile([P, PASSES * 512], BF16, name="w1_b3", align_bytes=64),
+        ]
+
+        nc.vector.memset(tab_s[:].bitcast(I32), 0)
+        nc.vector.memset(w4_s[:].bitcast(I32), 0)
+        nc.gpsimd.memset(vec_rows[:], 0.0)
+        make_identity(nc, ident[:])
+
+        def load_w1(tiles, c0, c1):
+            for a in range(PASSES):
+                nc.sync.dma_start(tiles[a][:], w1[512 * a : 512 * (a + 1), c0:c1].rearrange("(p i) c -> p i c", i=4))
+
+        def load_tab(a):
+            nc.sync.dma_start(tab_w[a][:], tab_words[a].rearrange("p t i -> p (t i)").bitcast(I32))
+
+        def rows(b):
+            return slice(P * b, P * (b + 1))
+
+        nc.sync.dma_start(idx1[:], offs)
+        load_tab(0)
+        for q in range(4):
+            nc.scalar.dma_start(
+                tab_s[32 * q : 32 * q + 4 * PASSES, :].bitcast(I32), tab_scales[:, 4 * q : 4 * q + 4, :].bitcast(I32)
+            )
+        load_tab(1)
+        load_w1(raw0, 0, P)
+        load_tab(2)
+        nc.sync.dma_start(vec_rows[0:BLOCKS, :], gain.rearrange("(b p) -> b p", p=P))
+        nc.sync.dma_start(vec_rows[BLOCKS : 2 * BLOCKS, :], knee.rearrange("(b p) -> b p", p=P))
+        nc.sync.dma_start(idx2[:], offs2)
+        nc.sync.dma_start(wgs_t[:, :HALF], wgs[:, :HALF])
+        nc.sync.dma_start(base_t[0][:, :HALF], base[rows(0), :HALF])
+        nc.sync.dma_start(pg0[0][:], page0[rows(0), :])
+        load_w1(raw1, P, 2 * P)
+        nc.sync.dma_start(wgs_t[:, HALF:], wgs[:, HALF:])
+        nc.sync.dma_start(base_t[0][:, HALF:], base[rows(0), HALF:])
+        nc.sync.dma_start(base_t[1][:], base[rows(1), :])
+        nc.sync.dma_start(idx3[:], offs3)
+        nc.sync.dma_start(pg0[1][:], page0[rows(1), :])
+        load_w1(raw23, 2 * P, 4 * P)
+        for b in (2, 3):
+            nc.sync.dma_start(base_t[b][:], base[rows(b), :])
+            nc.sync.dma_start(pg0[b][:], page0[rows(b), :])
+        nc.sync.dma_start(w4_w[:].bitcast(I32), w4_words[0].bitcast(I32))
+        for q in range(4):
+            nc.sync.dma_start(w4_s[32 * q : 32 * q + 4, :].bitcast(I32), w4_scales[0, 4 * q : 4 * q + 4, :].bitcast(I32))
+        nc.sync.dma_start(wgo_t[:], wgo)
+        nc.sync.dma_start(idx4[:], offs4)
+        for n in range(BLOCKS):
+            nc.sync.dma_start(pg1[n][:], page1[rows(n), :])
+
+        def cast_w1(b):
+            for a in range(PASSES):
+                src = (raw0, raw1, raw23, raw23)[b][a]
+                c0 = P if b == 3 else 0
+                nc.scalar.copy(
+                    w1_b[b][:, 512 * a : 512 * (a + 1)].rearrange("p (c j t) -> p c t j", j=4, t=4),
+                    src[:, :, c0 : c0 + P].rearrange("p t (c j) -> p c t j", j=4),
+                )
+
+        def quantise_w1(b):
+            for c0, c1 in ((0, 256), (256, 384)):
+                nc.vector.quantize_mx(w1_c[b][:, c0:c1].bitcast(FP8X4), w1_s[b][:, c0:c1], w1_b[b][:, 4 * c0 : 4 * c1])
+
+        def first_product(b, h):
+            cols = slice(HALF * h, HALF * (h + 1))
+            for a in range(PASSES):
+                nc.tensor.matmul_mx(
+                    bank[2 * (b % 2) + h][:],
+                    lhsT=w1_c[b][:, P * a : P * (a + 1)].bitcast(FP8X4),
+                    lhsT_scale=w1_s[b][:, P * a : P * (a + 1)],
+                    rhs=v_w[a][:, cols].bitcast(FP8X4),
+                    rhs_scale=v_s[4 * a : P, cols],
+                    start=(a == 0),
+                    stop=(a == PASSES - 1),
+                )
+
+        def scale_wgs(b, cols):
+            nc.scalar.activation(wg[b][:, cols], wgs_t[:, cols], ACT.Copy, scale=vec_cols[:, b : b + 1])
+
+        def add_base(b, h):
+            cols = slice(HALF * h, HALF * (h + 1))
+            nc.vector.tensor_tensor(base_t[b][:, cols], bank[2 * (b % 2) + h][:], base_t[b][:, cols], ADD)
+
+        def evacuate(dst, src):
+            nc.scalar.copy(dst, src)
+
+        def pool_op(dst, a, b, op):
+            nc.gpsimd.tensor_tensor(dst, a, b, op)
+
+        def put_plain(page, idx, cols, values):
+            nc.vector.tensor_copy(page[:].indirect(entries(idx, cols)), values)
+
+        def put_states(b, cols):
+            nc.vector.tensor_tensor(pg0[b][:].indirect(entries(idx2, cols)), base_t[b][:, cols], wg[b][:, cols], MULT)
+
+        def recall(b, cols, xr):
+            nc.vector.tensor_copy(xr, pg0[b][:].indirect(entries(idx3, cols)))
+
+        def damping(b, xr, r):
+            nc.scalar.activation(r, xr, ACT.Abs)
+            nc.scalar.activation(r, r, ACT.Abs_reciprocal_sqrt, bias=1.0, scale=vec_cols[:, BLOCKS + b : BLOCKS + b + 1])
+            nc.scalar.activation(r, r, ACT.Square)
+
+        def damp(x, xr, r):
+            nc.gpsimd.tensor_tensor(x, xr, r, MULT)
+
+        def turn(b, g, x, dst):
+            cols = GROUPS[g]
+            tiles = (cols.stop - cols.start) // P
+            for j in range(tiles):
+                nc.tensor.transpose(dst[:, P * j : P * (j + 1)], x[:, cols.start + P * j : cols.start + P * (j + 1)], ident[:])
+            nc.scalar.copy(
+                x_t[g][:].rearrange("p (j u q e) -> p j u q e", u=2, q=P, e=2)[:, :, :, 32 * b : 32 * (b + 1), :],
+                dst[:, : P * tiles].rearrange("p (j q u e) -> p j u q e", q=32, u=2, e=2),
+            )
+
+        def turn_back(g, dsts):
+            words = x_t[g][:].bitcast(F32)
+            woven = x_g[g][:].bitcast(F32)
+            for i, dst in enumerate(dsts):
+                for s in range(4):
+                    nc.tensor.transpose(dst[:, P * s : P * (s + 1)], words[:, 512 * i + P * s : 512 * i + P * (s + 1)], ident[:])
+                nc.scalar.copy(
+                    woven[:, 512 * i : 512 * (i + 1)].rearrange("p (j m u) -> p j m u", j=2, u=2),
+                    dst[:].rearrange("p (j u m) -> p j m u", j=2, u=2),
+                )
+
+        def quantise_x(g):
+            nc.vector.quantize_mx(x_c[g][:].bitcast(FP8X4), x_s[g][:], x_g[g][:])
+
+        def second_product(n, g, dst):
+            nc.tensor.matmul_mx(
+                dst,
+                lhsT=w4_w[:, 2 * P * n : 2 * P * (n + 1)].bitcast(FP4X4),
+                lhsT_scale=w4_s[:, rows(n)],
+                rhs=x_c[g][:].bitcast(FP8X4),
+                rhs_scale=x_s[g][:],
+                start=True,
+                stop=True,
+            )
+
+        def gate(x, g, src):
+            nc.vector.tensor_tensor(x[:, GROUPS[g]], src, x[:, GROUPS[g]], MULT)
+
+        def put_pulses(n, cols, y):
+            nc.vector.tensor_tensor(pg1[n][:].indirect(entries(idx4, cols)), y[:, cols], wgo_t[:, cols], MULT)
+
+        nc.vector.tensor_copy(v_s[:], tab_s[:].indirect(idx1[:]))
+        for a in range(PASSES - 1):
+            nc.vector.tensor_copy(v_w[a][:], tab_w[a][:].bitcast(U32).indirect(idx1[:]))
+        cast_w1(0)
+        quantise_w1(0)
+        halves = (slice(0, HALF), slice(HALF, S))
+        for cols in halves:
+            nc.vector.tensor_copy(v_w[2][:, cols], tab_w[2][:].bitcast(U32).indirect(entries(idx1, cols)))
+        nc.tensor.transpose(bank[4][:, :P], vec_rows[:], ident[:])
+        nc.scalar.copy(vec_cols[:], bank[4][:, : 2 * BLOCKS])
+        whole = slice(0, S)
+
+        scale_wgs(0, halves[0])
+        first_product(0, 0)
+        add_base(0, 0)
+        put_states(0, halves[0])
+        cast_w1(1)
+        quantise_w1(1)
+        scale_wgs(0, halves[1])
+        first_product(0, 1)
+        u0b = arena.tile([P, HALF], F32, name="u0b", offset=0)
+        nc.vector.tensor_tensor(u0b[:], bank[1][:], base_t[0][:, halves[1]], ADD)
+        nc.vector.tensor_tensor(pg0[0][:].indirect(entries(idx2, halves[1])), u0b[:], wg[0][:, halves[1]], MULT)
+
+        def states(b, h, dst):
+            cols = halves[h]
+            first_product(b, h)
+            evacuate(ebuf[:, cols], bank[2 * (b % 2) + h][:])
+            pool_op(base_t[b][:, cols], ebuf[:, cols], base_t[b][:, cols], ADD)
+            pool_op(dst, base_t[b][:, cols], wg[b][:, cols], MULT)
+
+        scale_wgs(1, whole)
+        states(1, 0, base_t[1][:, halves[0]])
+        cast_w1(2)
+        cast_w1(3)
+        scale_wgs(2, whole)
+        scale_wgs(3, whole)
+        for cols in (FIRST, REST):
+            recall(0, cols, xr0[:, cols])
+        put_plain(pg0[1], idx2, halves[0], base_t[1][:, halves[0]])
+        quantise_w1(2)
+        u1b = arena.tile([P, HALF], F32, name="u1b", offset=3072)
+        states(1, 1, u1b[:])
+        put_plain(pg0[1], idx2, halves[1], u1b[:])
+        quantise_w1(3)
+        for h in range(2):
+            states(2, h, base_t[2][:, halves[h]])
+        for h in range(2):
+            states(3, h, base_t[3][:, halves[h]])
+
+        rbuf0 = arena.tile([P, S], F32, name="rbuf0", offset=6144 + 4096 * 2)
+        x = [x0, wg[1], wg[2], wg[0]]
+
+        def weigh(b, cols):
+            pool_op(x[b][:, cols], x[b][:, cols], wgo_t[:, cols], MULT)
+
+        for cols in (FIRST, REST):
+            damping(0, xr0[:, cols], rbuf0[:, cols])
+        for cols in (FIRST, REST):
+            recall(1, cols, xr1[:, cols])
+        put_plain(pg0[2], idx2, whole, base_t[2][:])
+        for cols in (FIRST, REST):
+            damp(x[0][:, cols], xr0[:, cols], rbuf0[:, cols])
+        for cols in (FIRST, REST):
+            damping(1, xr1[:, cols], rbuf1[:, cols])
+        turn(0, 0, x[0], bank[4])
+        turn(0, 2, x[0], bank[5])
+        turn(0, 1, x[0], bank[4])
+        recall(2, FIRST, base_t[2][:, FIRST])
+        put_plain(pg0[3], idx2, whole, base_t[3][:])
+        for cols in (FIRST, REST):
+            damp(x[1][:, cols], xr1[:, cols], rbuf1[:, cols])
+        damping(2, base_t[2][:, FIRST], rbuf0[:, FIRST])
+        damp(x[2][:, FIRST], base_t[2][:, FIRST], rbuf0[:, FIRST])
+        turn(1, 0, x[1], bank[4])
+        turn(1, 2, x[1], bank[5])
+        turn(1, 1, x[1], bank[4])
+        turn(2, 0, x[2], bank[6])
+        weigh(0, whole)
+        weigh(2, FIRST)
+        weigh(1, whole)
+
+        recall(3, FIRST, base_t[1][:, FIRST])
+        damping(3, base_t[1][:, FIRST], xr0[:, FIRST])
+        damp(x[3][:, FIRST], base_t[1][:, FIRST], xr0[:, FIRST])
+        turn(3, 0, x[3], bank[3])
+        weigh(3, FIRST)
+        turn_back(0, [bank[6]])
+        quantise_x(0)
+        half_banks = [bank[i // 2][:, 256 * (i % 2) : 256 * (i % 2 + 1)] for i in range(8)]
+        for n in range(BLOCKS):
+            second_product(n, 0, half_banks[n])
+        for n in range(BLOCKS):
+            gate(x[n], 0, half_banks[n])
+        for n in range(BLOCKS):
+            put_plain(pg1[n], idx4, FIRST, x[n][:, FIRST])
+
+        recall(3, REST, base_t[1][:, REST])
+        damping(3, base_t[1][:, REST], xr0[:, REST])
+        recall(2, REST, base_t[3][:, REST])
+        damping(2, base_t[3][:, REST], rbuf0[:, REST])
+        damp(x[3][:, REST], base_t[1][:, REST], xr0[:, REST])
+        turn(3, 1, x[3], bank[4])
+        turn(3, 2, x[3], bank[5])
+        damp(x[2][:, REST], base_t[3][:, REST], rbuf0[:, REST])
+        turn(2, 1, x[2], bank[2])
+        turn(2, 2, x[2], bank[3])
+        turn_back(1, [bank[7]])
+        quantise_x(1)
+        turn_back(2, [bank[6], bank[7]])
+        quantise_x(2)
+        wide_banks = [bank[0], bank[1], bank[4], bank[5]]
+        sums = [wgs_t, rbuf1]
+        for n in range(BLOCKS):
+            second_product(n, 1, half_banks[4 + n])
+        for n in range(BLOCKS):
+            second_product(n, 2, wide_banks[n][:])
+        for n in range(BLOCKS):
+            if n >= 2:
+                weigh(n, REST)
+            evacuate(sums[n % 2][:, GROUPS[1]], half_banks[4 + n])
+            evacuate(sums[n % 2][:, GROUPS[2]], wide_banks[n][:])
+            pool_op(x[n][:, REST], sums[n % 2][:, REST], x[n][:, REST], MULT)
+            put_plain(pg1[n], idx4, REST, x[n][:, REST])
+            nc.sync.dma_start(out[rows(n), :], pg1[n][:])

@@ -50,26 +50,31 @@ def tile_list_patch_pulse_page_kernel(
 
         tab_w = [keep.tile([P, T], I32, name=f"tab_w{a}") for a in range(PASSES)]
         tab_s = keep.tile([P, T], U8, name="tab_s")
-        v_w = [keep.tile([P, S], U32, name=f"v_w{a}", align_bytes=64) for a in range(PASSES)]
+        base0_first = arena.tile([P, HALF], F32, name="base0_first", offset=38912)
+        v_w = [[keep.tile([P, HALF], U32, name=f"v_w{a}_{h}", align_bytes=64) for h in range(2) if (a, h) != (1, 1)] for a in range(PASSES)]
         v_s = keep.tile([P, S], U8, name="v_s", align_bytes=64)
-        raw0 = [keep.tile([P, 4, P], F32, name=f"raw0_{a}") for a in range(PASSES)]
-        raw1 = [keep.tile([P, 4, P], F32, name=f"raw1_{a}") for a in range(PASSES)]
-        raw23 = [arena.tile([P, 4, 2 * P], F32, name=f"raw23_{a}", offset=6144 + 4096 * a) for a in range(PASSES)]
+        raw_at = (0, 6144, 18432, 12288)
+        raw = [
+            [arena.tile([P, 4, P], F32, name=f"raw{b}_{a}", offset=raw_at[b] + 2048 * a) for a in range(PASSES)]
+            for b in range(BLOCKS)
+        ]
         w1_c = [keep.tile([P, PASSES * P], U32, name=f"w1_c{b}", align_bytes=64) for b in range(BLOCKS)]
         w1_s = [keep.tile([P, PASSES * P], U8, name=f"w1_s{b}", align_bytes=64) for b in range(BLOCKS)]
-        base_t = [keep.tile([P, S], F32, name=f"base{b}") for b in range(BLOCKS)]
+        base_t = [keep.tile([P, S], F32, name=f"base{b}") for b in range(BLOCKS - 1)]
+        base_t.append(arena.tile([P, S], F32, name="base3", offset=24576))
         wgs_t = keep.tile([P, S], F32, name="wgs_t")
-        wg = [keep.tile([P, S], F32, name=f"wg{b}") for b in range(BLOCKS)]
-        rbuf1 = keep.tile([P, S], F32, name="rbuf1")
-        ebuf = keep.tile([P, S], F32, name="ebuf")
-        x0 = keep.tile([P, S], F32, name="x0")
-        xr0 = keep.tile([P, S], F32, name="xr0")
-        xr1 = keep.tile([P, S], F32, name="xr1")
+        x = [keep.tile([P, BLOCKS * (g.stop - g.start)], F32, name=f"x{i}") for i, g in enumerate(GROUPS)]
+        wg = [x[0], x[1], x[2][:, :S], x[2][:, S:]]
+        sg_late = keep.tile([P, 2560], F32, name="sg_late")
+        ebuf = [keep.tile([P, S], F32, name=f"ebuf{i}") for i in range(2)]
         pg0 = [keep.tile([P, T], F32, name=f"pg0_{b}") for b in range(BLOCKS)]
         pg1 = [keep.tile([P, T], F32, name=f"pg1_{b}") for b in range(BLOCKS)]
         wgo_t = keep.tile([P, S], F32, name="wgo_t")
         x_t = [keep.tile([P, 4 * (g.stop - g.start)], BF16, name=f"x_t{i}") for i, g in enumerate(GROUPS)]
-        x_g = [keep.tile([P, 4 * (g.stop - g.start)], BF16, name=f"x_g{i}", align_bytes=64) for i, g in enumerate(GROUPS)]
+        x_g = [
+            arena.tile([P, 4 * (g.stop - g.start)], BF16, name=f"x_g{i}", align_bytes=64, offset=30720 + 8 * g.start)
+            for i, g in enumerate(GROUPS)
+        ]
         x_c = [keep.tile([P, g.stop - g.start], U32, name=f"x_c{i}", align_bytes=64) for i, g in enumerate(GROUPS)]
         x_s = [keep.tile([P, g.stop - g.start], U8, name=f"x_s{i}", align_bytes=64) for i, g in enumerate(GROUPS)]
         w4_w = keep.tile([P, 2 * H], U8, name="w4_w", align_bytes=64)
@@ -78,20 +83,22 @@ def tile_list_patch_pulse_page_kernel(
         vec_rows = keep.tile([P, P], F32, name="vec_rows")
         vec_cols = keep.tile([P, 2 * BLOCKS], F32, name="vec_cols")
         w1_b = [
-            keep.tile([P, PASSES * 512], BF16, name="w1_b0", align_bytes=64),
-            arena.tile([P, PASSES * 512], BF16, name="w1_b1", align_bytes=64, offset=0),
-            arena.tile([P, PASSES * 512], BF16, name="w1_b2", align_bytes=64, offset=3072),
-            keep.tile([P, PASSES * 512], BF16, name="w1_b3", align_bytes=64),
+            arena.tile([P, PASSES * 512], BF16, name=f"w1_b{b}", align_bytes=64, offset=40960 + 3072 * b)
+            for b in range(BLOCKS)
         ]
+        xr_first = keep.tile([P, HALF], F32, name="xr_first")
 
-        nc.vector.memset(tab_s[:].bitcast(I32), 0)
+        nc.gpsimd.memset(tab_s[:].bitcast(I32), 0)
         nc.vector.memset(w4_s[:].bitcast(I32), 0)
         nc.gpsimd.memset(vec_rows[:], 0.0)
         make_identity(nc, ident[:])
 
-        def load_w1(tiles, c0, c1):
+        warm = keep.tile([P, 1], F32, name="warm")
+        nc.scalar.activation(warm[:], ident[:, 0:1], ACT.Abs_reciprocal_sqrt, bias=1.0)
+
+        def load_w1(b):
             for a in range(PASSES):
-                nc.sync.dma_start(tiles[a][:], w1[512 * a : 512 * (a + 1), c0:c1].rearrange("(p i) c -> p i c", i=4))
+                nc.sync.dma_start(raw[b][a][:], w1[512 * a : 512 * (a + 1), P * b : P * (b + 1)].rearrange("(p i) c -> p i c", i=4))
 
         def load_tab(a):
             nc.sync.dma_start(tab_w[a][:], tab_words[a].rearrange("p t i -> p (t i)").bitcast(I32))
@@ -101,69 +108,63 @@ def tile_list_patch_pulse_page_kernel(
 
         nc.sync.dma_start(idx1[:], offs)
         load_tab(0)
+        load_tab(1)
         for q in range(4):
-            nc.scalar.dma_start(
+            nc.sync.dma_start(
                 tab_s[32 * q : 32 * q + 4 * PASSES, :].bitcast(I32), tab_scales[:, 4 * q : 4 * q + 4, :].bitcast(I32)
             )
-        load_tab(1)
-        load_w1(raw0, 0, P)
-        load_tab(2)
         nc.sync.dma_start(vec_rows[0:BLOCKS, :], gain.rearrange("(b p) -> b p", p=P))
         nc.sync.dma_start(vec_rows[BLOCKS : 2 * BLOCKS, :], knee.rearrange("(b p) -> b p", p=P))
+        load_w1(0)
+        load_tab(2)
         nc.sync.dma_start(idx2[:], offs2)
         nc.sync.dma_start(wgs_t[:, :HALF], wgs[:, :HALF])
-        nc.sync.dma_start(base_t[0][:, :HALF], base[rows(0), :HALF])
+        nc.sync.dma_start(base0_first[:], base[rows(0), :HALF])
         nc.sync.dma_start(pg0[0][:], page0[rows(0), :])
-        load_w1(raw1, P, 2 * P)
         nc.sync.dma_start(wgs_t[:, HALF:], wgs[:, HALF:])
         nc.sync.dma_start(base_t[0][:, HALF:], base[rows(0), HALF:])
+        load_w1(1)
         nc.sync.dma_start(base_t[1][:], base[rows(1), :])
+        load_w1(2)
         nc.sync.dma_start(idx3[:], offs3)
         nc.sync.dma_start(pg0[1][:], page0[rows(1), :])
-        load_w1(raw23, 2 * P, 4 * P)
-        for b in (2, 3):
-            nc.sync.dma_start(base_t[b][:], base[rows(b), :])
-            nc.sync.dma_start(pg0[b][:], page0[rows(b), :])
+        load_w1(3)
+        nc.sync.dma_start(base_t[2][:], base[rows(2), :])
+        nc.sync.dma_start(base_t[3][:], base[rows(3), :])
+        nc.sync.dma_start(wgo_t[:], wgo)
+        nc.sync.dma_start(pg0[2][:], page0[rows(2), :])
         nc.sync.dma_start(w4_w[:].bitcast(I32), w4_words[0].bitcast(I32))
         for q in range(4):
             nc.sync.dma_start(w4_s[32 * q : 32 * q + 4, :].bitcast(I32), w4_scales[0, 4 * q : 4 * q + 4, :].bitcast(I32))
-        nc.sync.dma_start(wgo_t[:], wgo)
         nc.sync.dma_start(idx4[:], offs4)
-        for n in range(BLOCKS):
-            nc.sync.dma_start(pg1[n][:], page1[rows(n), :])
+        for page, src, n in ((pg1, page1, 0), (pg1, page1, 1), (pg0, page0, 3), (pg1, page1, 3), (pg1, page1, 2)):
+            nc.sync.dma_start(page[n][:], src[rows(n), :])
 
         def cast_w1(b):
             for a in range(PASSES):
-                src = (raw0, raw1, raw23, raw23)[b][a]
-                c0 = P if b == 3 else 0
                 nc.scalar.copy(
                     w1_b[b][:, 512 * a : 512 * (a + 1)].rearrange("p (c j t) -> p c t j", j=4, t=4),
-                    src[:, :, c0 : c0 + P].rearrange("p t (c j) -> p c t j", j=4),
+                    raw[b][a][:].rearrange("p t (c j) -> p c t j", j=4),
                 )
 
         def quantise_w1(b):
             for c0, c1 in ((0, 256), (256, 384)):
                 nc.vector.quantize_mx(w1_c[b][:, c0:c1].bitcast(FP8X4), w1_s[b][:, c0:c1], w1_b[b][:, 4 * c0 : 4 * c1])
 
-        def first_product(b, h):
-            cols = slice(HALF * h, HALF * (h + 1))
+        def first_product(b, cols, dst):
             for a in range(PASSES):
                 nc.tensor.matmul_mx(
-                    bank[2 * (b % 2) + h][:],
+                    dst,
                     lhsT=w1_c[b][:, P * a : P * (a + 1)].bitcast(FP8X4),
                     lhsT_scale=w1_s[b][:, P * a : P * (a + 1)],
-                    rhs=v_w[a][:, cols].bitcast(FP8X4),
+                    rhs=v_w[a][cols.start // HALF][:, cols.start % HALF : cols.start % HALF + cols.stop - cols.start].bitcast(FP8X4),
                     rhs_scale=v_s[4 * a : P, cols],
                     start=(a == 0),
                     stop=(a == PASSES - 1),
                 )
 
         def scale_wgs(b, cols):
-            nc.scalar.activation(wg[b][:, cols], wgs_t[:, cols], ACT.Copy, scale=vec_cols[:, b : b + 1])
-
-        def add_base(b, h):
-            cols = slice(HALF * h, HALF * (h + 1))
-            nc.vector.tensor_tensor(base_t[b][:, cols], bank[2 * (b % 2) + h][:], base_t[b][:, cols], ADD)
+            nc.gpsimd.tensor_scalar(wg[b][:, cols], wgs_t[:, cols], vec_cols[:, b : b + 1], 0.0, MULT, ADD)
 
         def evacuate(dst, src):
             nc.scalar.copy(dst, src)
@@ -174,37 +175,37 @@ def tile_list_patch_pulse_page_kernel(
         def put_plain(page, idx, cols, values):
             nc.vector.tensor_copy(page[:].indirect(entries(idx, cols)), values)
 
-        def put_states(b, cols):
-            nc.vector.tensor_tensor(pg0[b][:].indirect(entries(idx2, cols)), base_t[b][:, cols], wg[b][:, cols], MULT)
-
         def recall(b, cols, xr):
             nc.vector.tensor_copy(xr, pg0[b][:].indirect(entries(idx3, cols)))
 
-        def damping(b, xr, r):
+        def damped(blocks, xr, r, sg, into):
+            width = xr.shape[1] // len(blocks)
             nc.scalar.activation(r, xr, ACT.Abs)
-            nc.scalar.activation(r, r, ACT.Abs_reciprocal_sqrt, bias=1.0, scale=vec_cols[:, BLOCKS + b : BLOCKS + b + 1])
+            for i, b in enumerate(blocks):
+                cols = slice(width * i, width * (i + 1))
+                knee_b = vec_cols[:, BLOCKS + b : BLOCKS + b + 1]
+                nc.scalar.activation(sg[:, cols], r[:, cols], ACT.Sign, bias=1.0, scale=knee_b)
+                nc.scalar.activation(r[:, cols], r[:, cols], ACT.Abs_reciprocal_sqrt, bias=1.0, scale=knee_b)
             nc.scalar.activation(r, r, ACT.Square)
-
-        def damp(x, xr, r):
-            nc.gpsimd.tensor_tensor(x, xr, r, MULT)
+            pool_op(xr, xr, sg, MULT)
+            pool_op(into, xr, r, MULT)
 
         def turn(b, g, x, dst):
-            cols = GROUPS[g]
-            tiles = (cols.stop - cols.start) // P
+            tiles = (GROUPS[g].stop - GROUPS[g].start) // P
             for j in range(tiles):
-                nc.tensor.transpose(dst[:, P * j : P * (j + 1)], x[:, cols.start + P * j : cols.start + P * (j + 1)], ident[:])
+                nc.tensor.transpose(dst[:, P * j : P * (j + 1)], x[:, P * j : P * (j + 1)], ident[:])
             nc.scalar.copy(
                 x_t[g][:].rearrange("p (j u q e) -> p j u q e", u=2, q=P, e=2)[:, :, :, 32 * b : 32 * (b + 1), :],
                 dst[:, : P * tiles].rearrange("p (j q u e) -> p j u q e", q=32, u=2, e=2),
             )
 
-        def turn_back(g, dsts):
+        def turn_back(g, dsts, copy):
             words = x_t[g][:].bitcast(F32)
             woven = x_g[g][:].bitcast(F32)
             for i, dst in enumerate(dsts):
                 for s in range(4):
                     nc.tensor.transpose(dst[:, P * s : P * (s + 1)], words[:, 512 * i + P * s : 512 * i + P * (s + 1)], ident[:])
-                nc.scalar.copy(
+                copy(
                     woven[:, 512 * i : 512 * (i + 1)].rearrange("p (j m u) -> p j m u", j=2, u=2),
                     dst[:].rearrange("p (j u m) -> p j m u", j=2, u=2),
                 )
@@ -223,134 +224,146 @@ def tile_list_patch_pulse_page_kernel(
                 stop=True,
             )
 
-        def gate(x, g, src):
-            nc.vector.tensor_tensor(x[:, GROUPS[g]], src, x[:, GROUPS[g]], MULT)
+        halves = (slice(0, HALF), slice(HALF, S))
+        quarters = [slice(256 * i, 256 * (i + 1)) for i in range(4)]
 
-        def put_pulses(n, cols, y):
-            nc.vector.tensor_tensor(pg1[n][:].indirect(entries(idx4, cols)), y[:, cols], wgo_t[:, cols], MULT)
+        def pick(a, h):
+            nc.vector.tensor_copy(v_w[a][h][:], tab_w[a][:].bitcast(U32).indirect(entries(idx1, halves[h])))
 
+        pick(0, 0)
         nc.vector.tensor_copy(v_s[:], tab_s[:].indirect(idx1[:]))
-        for a in range(PASSES - 1):
-            nc.vector.tensor_copy(v_w[a][:], tab_w[a][:].bitcast(U32).indirect(idx1[:]))
+        pick(1, 0)
         cast_w1(0)
         quantise_w1(0)
-        halves = (slice(0, HALF), slice(HALF, S))
-        for cols in halves:
-            nc.vector.tensor_copy(v_w[2][:, cols], tab_w[2][:].bitcast(U32).indirect(entries(idx1, cols)))
+        pick(2, 0)
         nc.tensor.transpose(bank[4][:, :P], vec_rows[:], ident[:])
         nc.scalar.copy(vec_cols[:], bank[4][:, : 2 * BLOCKS])
-        whole = slice(0, S)
-
         scale_wgs(0, halves[0])
-        first_product(0, 0)
-        add_base(0, 0)
-        put_states(0, halves[0])
+        first_product(0, halves[0], bank[0][:])
+        nc.vector.tensor_tensor(base_t[0][:, halves[0]], bank[0][:], base0_first[:], ADD)
+        pool_op(base_t[0][:, halves[0]], base_t[0][:, halves[0]], wg[0][:, halves[0]], MULT)
+        put_plain(pg0[0], idx2, halves[0], base_t[0][:, halves[0]])
+        v_w[1].append(arena.tile([P, HALF], U32, name="v_w1_1", align_bytes=64, offset=38912))
+        for a in range(PASSES):
+            pick(a, 1)
+
+        def states(b, cols, dst, into=None):
+            into = base_t[b][:, cols] if into is None else into
+            first_product(b, cols, dst)
+            evacuate(sums[b][:, cols], dst)
+            pool_op(base_t[b][:, cols], sums[b][:, cols], base_t[b][:, cols], ADD)
+            pool_op(into, base_t[b][:, cols], wg[b][:, cols], MULT)
+            put_plain(pg0[b], idx2, cols, into)
+
+        def x_of(g, b, count=1):
+            width = GROUPS[g].stop - GROUPS[g].start
+            return x[g][:, width * b : width * (b + count)]
+
+        def weigh(g, b, count=1, src=None):
+            width = GROUPS[g].stop - GROUPS[g].start
+            src = x_of(g, b, count) if src is None else src
+            nc.gpsimd.tensor_tensor(
+                x_of(g, b, count).rearrange("p (n c) -> p n c", n=count),
+                src.rearrange("p (n c) -> p n c", n=count),
+                wgo_t[:, GROUPS[g]].unsqueeze(1).to_broadcast([P, count, width]),
+                MULT,
+            )
+
+        def make_x(g, blocks, xr, r, sg, banks, into=None):
+            width = GROUPS[g].stop - GROUPS[g].start
+            into = x_of(g, blocks[0], len(blocks)) if into is None else into
+            for i, b in enumerate(blocks):
+                recall(b, GROUPS[g], xr[:, width * i : width * (i + 1)])
+            damped(blocks, xr, r, sg, into)
+            for i, b in enumerate(blocks):
+                turn(b, g, into[:, width * i : width * (i + 1)], banks[i])
+
+        sums = [ebuf[0]]
         cast_w1(1)
         quantise_w1(1)
         scale_wgs(0, halves[1])
-        first_product(0, 1)
-        u0b = arena.tile([P, HALF], F32, name="u0b", offset=0)
-        nc.vector.tensor_tensor(u0b[:], bank[1][:], base_t[0][:, halves[1]], ADD)
-        nc.vector.tensor_tensor(pg0[0][:].indirect(entries(idx2, halves[1])), u0b[:], wg[0][:, halves[1]], MULT)
-
-        def states(b, h, dst):
-            cols = halves[h]
-            first_product(b, h)
-            evacuate(ebuf[:, cols], bank[2 * (b % 2) + h][:])
-            pool_op(base_t[b][:, cols], ebuf[:, cols], base_t[b][:, cols], ADD)
-            pool_op(dst, base_t[b][:, cols], wg[b][:, cols], MULT)
-
-        scale_wgs(1, whole)
-        states(1, 0, base_t[1][:, halves[0]])
-        cast_w1(2)
-        cast_w1(3)
-        scale_wgs(2, whole)
-        scale_wgs(3, whole)
-        for cols in (FIRST, REST):
-            recall(0, cols, xr0[:, cols])
-        put_plain(pg0[1], idx2, halves[0], base_t[1][:, halves[0]])
-        quantise_w1(2)
-        u1b = arena.tile([P, HALF], F32, name="u1b", offset=3072)
-        states(1, 1, u1b[:])
-        put_plain(pg0[1], idx2, halves[1], u1b[:])
-        quantise_w1(3)
-        for h in range(2):
-            states(2, h, base_t[2][:, halves[h]])
-        for h in range(2):
-            states(3, h, base_t[3][:, halves[h]])
-
-        rbuf0 = arena.tile([P, S], F32, name="rbuf0", offset=6144 + 4096 * 2)
-        x = [x0, wg[1], wg[2], wg[0]]
-
-        def weigh(b, cols):
-            pool_op(x[b][:, cols], x[b][:, cols], wgo_t[:, cols], MULT)
-
-        for cols in (FIRST, REST):
-            damping(0, xr0[:, cols], rbuf0[:, cols])
-        for cols in (FIRST, REST):
-            recall(1, cols, xr1[:, cols])
-        put_plain(pg0[2], idx2, whole, base_t[2][:])
-        for cols in (FIRST, REST):
-            damp(x[0][:, cols], xr0[:, cols], rbuf0[:, cols])
-        for cols in (FIRST, REST):
-            damping(1, xr1[:, cols], rbuf1[:, cols])
-        turn(0, 0, x[0], bank[4])
-        turn(0, 2, x[0], bank[5])
-        turn(0, 1, x[0], bank[4])
-        recall(2, FIRST, base_t[2][:, FIRST])
-        put_plain(pg0[3], idx2, whole, base_t[3][:])
-        for cols in (FIRST, REST):
-            damp(x[1][:, cols], xr1[:, cols], rbuf1[:, cols])
-        damping(2, base_t[2][:, FIRST], rbuf0[:, FIRST])
-        damp(x[2][:, FIRST], base_t[2][:, FIRST], rbuf0[:, FIRST])
-        turn(1, 0, x[1], bank[4])
-        turn(1, 2, x[1], bank[5])
-        turn(1, 1, x[1], bank[4])
-        turn(2, 0, x[2], bank[6])
-        weigh(0, whole)
-        weigh(2, FIRST)
-        weigh(1, whole)
-
-        recall(3, FIRST, base_t[1][:, FIRST])
-        damping(3, base_t[1][:, FIRST], xr0[:, FIRST])
-        damp(x[3][:, FIRST], base_t[1][:, FIRST], xr0[:, FIRST])
-        turn(3, 0, x[3], bank[3])
-        weigh(3, FIRST)
-        turn_back(0, [bank[6]])
+        h_third = arena.tile([P, 256], F32, name="h_third", offset=40960 + 3072)
+        first_product(0, quarters[2], bank[1][:, :256])
+        nc.vector.tensor_tensor(h_third[:], bank[1][:, :256], base_t[0][:, quarters[2]], ADD)
+        nc.vector.tensor_tensor(pg0[0][:].indirect(entries(idx2, quarters[2])), h_third[:], wg[0][:, quarters[2]], MULT)
+        states(0, quarters[3], bank[5][:, :256])
+        for b in (1, 2, 3):
+            scale_wgs(b, slice(0, S))
+        for b in (2, 3):
+            cast_w1(b)
+            quantise_w1(b)
+        sums.append(arena.tile([P, S], F32, name="sums1", offset=20480))
+        sums.append(arena.tile([P, S], F32, name="sums2", offset=13312))
+        sums.append(ebuf[1])
+        for i in range(4):
+            states(1, quarters[i], bank[(2, 3, 6, 7)[i]][:, :256])
+        for b in (2, 3):
+            for h, cols in enumerate(halves):
+                states(b, cols, bank[2 * (b % 2) + h][:])
+        r_first = arena.tile([P, 768 + HALF], F32, name="r_first", offset=12288)
+        make_x(0, (0,), xr_first[:, quarters[0]], r_first[:, quarters[0]], sg_late[:, quarters[0]], [bank[4]])
+        make_x(0, (1,), xr_first[:, quarters[1]], r_first[:, quarters[1]], sg_late[:, quarters[1]], [bank[5]])
+        weigh(0, 0, 2)
+        make_x(2, (0,), base_t[1][:, halves[1]], r_first[:, 768:], sg_late[:, 1024:1536], [bank[6]])
+        xr_two = arena.tile([P, 256], F32, name="xr_two", offset=17920)
+        make_x(0, (2,), xr_two[:], base_t[0][:, quarters[1]], sg_late[:, quarters[2]], [bank[4]])
+        xr_three = arena.tile([P, 256], F32, name="xr_three", offset=17408)
+        make_x(0, (3,), xr_three[:], r_first[:, quarters[2]], sg_late[:, quarters[3]], [bank[5]])
+        weigh(0, 2, 2)
+        turn_back(0, [bank[6]], nc.vector.tensor_copy)
         quantise_x(0)
-        half_banks = [bank[i // 2][:, 256 * (i % 2) : 256 * (i % 2 + 1)] for i in range(8)]
-        for n in range(BLOCKS):
-            second_product(n, 0, half_banks[n])
-        for n in range(BLOCKS):
-            gate(x[n], 0, half_banks[n])
-        for n in range(BLOCKS):
-            put_plain(pg1[n], idx4, FIRST, x[n][:, FIRST])
 
-        recall(3, REST, base_t[1][:, REST])
-        damping(3, base_t[1][:, REST], xr0[:, REST])
-        recall(2, REST, base_t[3][:, REST])
-        damping(2, base_t[3][:, REST], rbuf0[:, REST])
-        damp(x[3][:, REST], base_t[1][:, REST], xr0[:, REST])
-        turn(3, 1, x[3], bank[4])
-        turn(3, 2, x[3], bank[5])
-        damp(x[2][:, REST], base_t[3][:, REST], rbuf0[:, REST])
-        turn(2, 1, x[2], bank[2])
-        turn(2, 2, x[2], bank[3])
-        turn_back(1, [bank[7]])
+        def pulses(g, n, src, count=1):
+            width = GROUPS[g].stop - GROUPS[g].start
+            staged = ebuf[n % 2][:, GROUPS[g].start : GROUPS[g].start + width * count]
+            evacuate(staged, src)
+            pool_op(x_of(g, n, count), staged, x_of(g, n, count), MULT)
+            for m in range(n, n + count):
+                put_plain(pg1[m], idx4, GROUPS[g], x_of(g, m))
+
+        def pulses_direct(g, n, src, dst):
+            nc.vector.tensor_tensor(dst, src, x_of(g, n), MULT)
+            put_plain(pg1[n], idx4, GROUPS[g], dst)
+
+        xr_late = arena.tile([P, 2560], F32, name="xr_late", offset=18432)
+        xr_last = arena.tile([P, HALF], F32, name="xr_last", offset=30720)
+        r_late = arena.tile([P, 3072], F32, name="r_late", offset=0)
+
+        for n in range(BLOCKS):
+            second_product(n, 0, bank[n][:, :256])
+        pulses_direct(0, 0, bank[0][:, :256], x_of(0, 0))
+        pulses_direct(0, 1, bank[1][:, :256], x_of(0, 1))
+        pulses_direct(0, 3, bank[3][:, :256], x_of(0, 3))
+        make_x(1, (0,), xr_late[:, 0:256], r_late[:, 0:256], sg_late[:, 0:256], [bank[4], bank[5]])
+        make_x(1, (1,), xr_late[:, 256:512], r_late[:, 256:512], sg_late[:, 256:512], [bank[4], bank[5]][1:])
+        make_x(1, (2,), xr_late[:, 512:768], r_late[:, 512:768], sg_late[:, 512:768], [bank[4], bank[5]])
+        make_x(1, (3,), xr_late[:, 768:1024], r_late[:, 768:1024], sg_late[:, 768:1024], [bank[4], bank[5]][1:])
+        turn_back(1, [bank[7]], nc.scalar.copy)
         quantise_x(1)
-        turn_back(2, [bank[6], bank[7]])
+        y_a = arena.tile([P, 256], F32, name="y_a", offset=30720 + 8 * GROUPS[1].start)
+        pulses_direct(0, 2, bank[2][:, :256], y_a[:])
+        for n in range(BLOCKS):
+            second_product(n, 1, bank[n][:, 256:])
+        weigh(1, 0, 2)
+        pulses_direct(1, 0, bank[0][:, 256:], x_of(1, 0))
+        pulses_direct(1, 1, bank[1][:, 256:], x_of(1, 1))
+        make_x(2, (1,), xr_late[:, 1536:2048], r_late[:, 1536:2048], sg_late[:, 1536:2048], [bank[5]])
+        make_x(2, (2,), xr_late[:, 2048:2560], r_late[:, 2048:2560], sg_late[:, 2048:2560], [bank[4]])
+        make_x(2, (3,), xr_last[:], r_late[:, 2560:], sg_late[:, :HALF], [bank[5]])
+        turn_back(2, [bank[6], bank[7]], nc.scalar.copy)
         quantise_x(2)
-        wide_banks = [bank[0], bank[1], bank[4], bank[5]]
-        sums = [wgs_t, rbuf1]
+        y_b = arena.tile([P, 256], F32, name="y_b", offset=30720 + 8 * GROUPS[2].start)
+        weigh(1, 2, 2)
+        pulses_direct(1, 2, bank[2][:, 256:], y_b[:])
+        pulses_direct(1, 3, bank[3][:, 256:], x_of(1, 3))
+        weigh(2, 0, 4)
         for n in range(BLOCKS):
-            second_product(n, 1, half_banks[4 + n])
-        for n in range(BLOCKS):
-            second_product(n, 2, wide_banks[n][:])
-        for n in range(BLOCKS):
-            if n >= 2:
-                weigh(n, REST)
-            evacuate(sums[n % 2][:, GROUPS[1]], half_banks[4 + n])
-            evacuate(sums[n % 2][:, GROUPS[2]], wide_banks[n][:])
-            pool_op(x[n][:, REST], sums[n % 2][:, REST], x[n][:, REST], MULT)
-            put_plain(pg1[n], idx4, REST, x[n][:, REST])
-            nc.sync.dma_start(out[rows(n), :], pg1[n][:])
+            second_product(n, 2, bank[(0, 1, 4, 5)[n]][:])
+        pulses(2, 0, bank[0][:])
+        nc.sync.dma_start(out[rows(0), :], pg1[0][:])
+        pulses(2, 1, bank[1][:])
+        nc.sync.dma_start(out[rows(1), :], pg1[1][:])
+        pulses(2, 2, bank[4][:])
+        nc.sync.dma_start(out[rows(2), :], pg1[2][:])
+        pulses(2, 3, bank[5][:])
+        nc.sync.dma_start(out[rows(3), :], pg1[3][:])

@@ -50,8 +50,7 @@ def tile_list_patch_pulse_page_kernel(
 
         tab_w = [keep.tile([P, T], I32, name=f"tab_w{a}") for a in range(PASSES)]
         tab_s = keep.tile([P, T], U8, name="tab_s")
-        base0_first = arena.tile([P, HALF], F32, name="base0_first", offset=38912)
-        v_w = [[keep.tile([P, HALF], U32, name=f"v_w{a}_{h}", align_bytes=64) for h in range(2) if (a, h) != (1, 1)] for a in range(PASSES)]
+        v_w = [keep.tile([P, S], U32, name=f"v_w{a}", align_bytes=64) for a in range(PASSES)]
         v_s = keep.tile([P, S], U8, name="v_s", align_bytes=64)
         raw_at = (0, 6144, 18432, 12288)
         raw = [
@@ -65,8 +64,9 @@ def tile_list_patch_pulse_page_kernel(
         wgs_t = keep.tile([P, S], F32, name="wgs_t")
         x = [keep.tile([P, BLOCKS * (g.stop - g.start)], F32, name=f"x{i}") for i, g in enumerate(GROUPS)]
         wg = [x[0], x[1], x[2][:, :S], x[2][:, S:]]
+        base2_given = keep.tile([P, S], F32, name="base2_given")
         sg_late = keep.tile([P, 2560], F32, name="sg_late")
-        ebuf = [keep.tile([P, S], F32, name=f"ebuf{i}") for i in range(2)]
+        ebuf = [base_t[1], base_t[2]]
         pg0 = [keep.tile([P, T], F32, name=f"pg0_{b}") for b in range(BLOCKS)]
         pg1 = [keep.tile([P, T], F32, name=f"pg1_{b}") for b in range(BLOCKS)]
         wgo_t = keep.tile([P, S], F32, name="wgo_t")
@@ -82,11 +82,8 @@ def tile_list_patch_pulse_page_kernel(
         ident = keep.tile([P, P], F32, name="ident")
         vec_rows = keep.tile([P, P], F32, name="vec_rows")
         vec_cols = keep.tile([P, 2 * BLOCKS], F32, name="vec_cols")
-        w1_b = [
-            arena.tile([P, PASSES * 512], BF16, name=f"w1_b{b}", align_bytes=64, offset=40960 + 3072 * b)
-            for b in range(BLOCKS)
-        ]
-        xr_first = keep.tile([P, HALF], F32, name="xr_first")
+        w1_b = [keep.tile([P, PASSES * 512], BF16, name=f"w1_b{b}", align_bytes=64) for b in range(BLOCKS)]
+        xr_zero = keep.tile([P, S], F32, name="xr_zero")
 
         nc.gpsimd.memset(tab_s[:].bitcast(I32), 0)
         nc.vector.memset(w4_s[:].bitcast(I32), 0)
@@ -113,30 +110,29 @@ def tile_list_patch_pulse_page_kernel(
             nc.sync.dma_start(
                 tab_s[32 * q : 32 * q + 4 * PASSES, :].bitcast(I32), tab_scales[:, 4 * q : 4 * q + 4, :].bitcast(I32)
             )
-        nc.sync.dma_start(vec_rows[0:BLOCKS, :], gain.rearrange("(b p) -> b p", p=P))
-        nc.sync.dma_start(vec_rows[BLOCKS : 2 * BLOCKS, :], knee.rearrange("(b p) -> b p", p=P))
         load_w1(0)
         load_tab(2)
+        nc.sync.dma_start(vec_rows[0:BLOCKS, :], gain.rearrange("(b p) -> b p", p=P))
+        nc.sync.dma_start(vec_rows[BLOCKS : 2 * BLOCKS, :], knee.rearrange("(b p) -> b p", p=P))
         nc.sync.dma_start(idx2[:], offs2)
         nc.sync.dma_start(wgs_t[:, :HALF], wgs[:, :HALF])
-        nc.sync.dma_start(base0_first[:], base[rows(0), :HALF])
+        nc.sync.dma_start(base_t[0][:], base[rows(0), :])
         nc.sync.dma_start(pg0[0][:], page0[rows(0), :])
-        nc.sync.dma_start(wgs_t[:, HALF:], wgs[:, HALF:])
-        nc.sync.dma_start(base_t[0][:, HALF:], base[rows(0), HALF:])
         load_w1(1)
+        nc.sync.dma_start(wgs_t[:, HALF:], wgs[:, HALF:])
         nc.sync.dma_start(base_t[1][:], base[rows(1), :])
         load_w1(2)
         nc.sync.dma_start(idx3[:], offs3)
         nc.sync.dma_start(pg0[1][:], page0[rows(1), :])
         load_w1(3)
-        nc.sync.dma_start(base_t[2][:], base[rows(2), :])
-        nc.sync.dma_start(base_t[3][:], base[rows(3), :])
-        nc.sync.dma_start(wgo_t[:], wgo)
-        nc.sync.dma_start(pg0[2][:], page0[rows(2), :])
         nc.sync.dma_start(w4_w[:].bitcast(I32), w4_words[0].bitcast(I32))
         for q in range(4):
             nc.sync.dma_start(w4_s[32 * q : 32 * q + 4, :].bitcast(I32), w4_scales[0, 4 * q : 4 * q + 4, :].bitcast(I32))
         nc.sync.dma_start(idx4[:], offs4)
+        nc.sync.dma_start(wgo_t[:], wgo)
+        nc.sync.dma_start(base2_given[:], base[rows(2), :])
+        nc.sync.dma_start(base_t[3][:], base[rows(3), :])
+        nc.sync.dma_start(pg0[2][:], page0[rows(2), :])
         for page, src, n in ((pg1, page1, 0), (pg1, page1, 1), (pg0, page0, 3), (pg1, page1, 3), (pg1, page1, 2)):
             nc.sync.dma_start(page[n][:], src[rows(n), :])
 
@@ -157,14 +153,14 @@ def tile_list_patch_pulse_page_kernel(
                     dst,
                     lhsT=w1_c[b][:, P * a : P * (a + 1)].bitcast(FP8X4),
                     lhsT_scale=w1_s[b][:, P * a : P * (a + 1)],
-                    rhs=v_w[a][cols.start // HALF][:, cols.start % HALF : cols.start % HALF + cols.stop - cols.start].bitcast(FP8X4),
+                    rhs=v_w[a][:, cols].bitcast(FP8X4),
                     rhs_scale=v_s[4 * a : P, cols],
                     start=(a == 0),
                     stop=(a == PASSES - 1),
                 )
 
         def scale_wgs(b, cols):
-            nc.gpsimd.tensor_scalar(wg[b][:, cols], wgs_t[:, cols], vec_cols[:, b : b + 1], 0.0, MULT, ADD)
+            nc.scalar.activation(wg[b][:, cols], wgs_t[:, cols], ACT.Copy, scale=vec_cols[:, b : b + 1])
 
         def evacuate(dst, src):
             nc.scalar.copy(dst, src)
@@ -227,33 +223,15 @@ def tile_list_patch_pulse_page_kernel(
         halves = (slice(0, HALF), slice(HALF, S))
         quarters = [slice(256 * i, 256 * (i + 1)) for i in range(4)]
 
-        def pick(a, h):
-            nc.vector.tensor_copy(v_w[a][h][:], tab_w[a][:].bitcast(U32).indirect(entries(idx1, halves[h])))
+        whole = slice(0, S)
 
-        pick(0, 0)
-        nc.vector.tensor_copy(v_s[:], tab_s[:].indirect(idx1[:]))
-        pick(1, 0)
-        cast_w1(0)
-        quantise_w1(0)
-        pick(2, 0)
-        nc.tensor.transpose(bank[4][:, :P], vec_rows[:], ident[:])
-        nc.scalar.copy(vec_cols[:], bank[4][:, : 2 * BLOCKS])
-        scale_wgs(0, halves[0])
-        first_product(0, halves[0], bank[0][:])
-        nc.vector.tensor_tensor(base_t[0][:, halves[0]], bank[0][:], base0_first[:], ADD)
-        pool_op(base_t[0][:, halves[0]], base_t[0][:, halves[0]], wg[0][:, halves[0]], MULT)
-        put_plain(pg0[0], idx2, halves[0], base_t[0][:, halves[0]])
-        v_w[1].append(arena.tile([P, HALF], U32, name="v_w1_1", align_bytes=64, offset=38912))
-        for a in range(PASSES):
-            pick(a, 1)
+        def pick(a, cols):
+            nc.vector.tensor_copy(v_w[a][:, cols], tab_w[a][:].bitcast(U32).indirect(entries(idx1, cols)))
 
-        def states(b, cols, dst, into=None):
-            into = base_t[b][:, cols] if into is None else into
-            first_product(b, cols, dst)
-            evacuate(sums[b][:, cols], dst)
-            pool_op(base_t[b][:, cols], sums[b][:, cols], base_t[b][:, cols], ADD)
-            pool_op(into, base_t[b][:, cols], wg[b][:, cols], MULT)
-            put_plain(pg0[b], idx2, cols, into)
+        def add_base(b, given):
+            for h, cols in enumerate(halves):
+                first_product(b, cols, bank[2 * (b % 2) + h][:])
+                nc.vector.tensor_tensor(base_t[b][:, cols], bank[2 * (b % 2) + h][:], given[:, cols], ADD)
 
         def x_of(g, b, count=1):
             width = GROUPS[g].stop - GROUPS[g].start
@@ -272,43 +250,50 @@ def tile_list_patch_pulse_page_kernel(
         def make_x(g, blocks, xr, r, sg, banks, into=None):
             width = GROUPS[g].stop - GROUPS[g].start
             into = x_of(g, blocks[0], len(blocks)) if into is None else into
-            for i, b in enumerate(blocks):
-                recall(b, GROUPS[g], xr[:, width * i : width * (i + 1)])
             damped(blocks, xr, r, sg, into)
             for i, b in enumerate(blocks):
                 turn(b, g, into[:, width * i : width * (i + 1)], banks[i])
 
-        sums = [ebuf[0]]
+        pick(0, whole)
+        pick(1, whole)
+        nc.vector.tensor_copy(v_s[:], tab_s[:].indirect(idx1[:]))
+        cast_w1(0)
+        quantise_w1(0)
+        for cols in halves:
+            pick(2, cols)
+        nc.tensor.transpose(bank[4][:, :P], vec_rows[:], ident[:])
+        nc.scalar.copy(vec_cols[:], bank[4][:, : 2 * BLOCKS])
+        add_base(0, base_t[0])
         cast_w1(1)
         quantise_w1(1)
-        scale_wgs(0, halves[1])
-        h_third = arena.tile([P, 256], F32, name="h_third", offset=40960 + 3072)
-        first_product(0, quarters[2], bank[1][:, :256])
-        nc.vector.tensor_tensor(h_third[:], bank[1][:, :256], base_t[0][:, quarters[2]], ADD)
-        nc.vector.tensor_tensor(pg0[0][:].indirect(entries(idx2, quarters[2])), h_third[:], wg[0][:, quarters[2]], MULT)
-        states(0, quarters[3], bank[5][:, :256])
+        for cols in halves:
+            scale_wgs(0, cols)
+            nc.vector.tensor_tensor(pg0[0][:].indirect(entries(idx2, cols)), base_t[0][:, cols], wg[0][:, cols], MULT)
         for b in (1, 2, 3):
-            scale_wgs(b, slice(0, S))
+            scale_wgs(b, whole)
         for b in (2, 3):
             cast_w1(b)
             quantise_w1(b)
-        sums.append(arena.tile([P, S], F32, name="sums1", offset=20480))
-        sums.append(arena.tile([P, S], F32, name="sums2", offset=13312))
-        sums.append(ebuf[1])
-        for i in range(4):
-            states(1, quarters[i], bank[(2, 3, 6, 7)[i]][:, :256])
-        for b in (2, 3):
-            for h, cols in enumerate(halves):
-                states(b, cols, bank[2 * (b % 2) + h][:])
-        r_first = arena.tile([P, 768 + HALF], F32, name="r_first", offset=12288)
-        make_x(0, (0,), xr_first[:, quarters[0]], r_first[:, quarters[0]], sg_late[:, quarters[0]], [bank[4]])
-        make_x(0, (1,), xr_first[:, quarters[1]], r_first[:, quarters[1]], sg_late[:, quarters[1]], [bank[5]])
+        for b in (1, 2, 3):
+            add_base(b, base2_given if b == 2 else base_t[b])
+            for cols in halves:
+                pool_op(base_t[b][:, cols], base_t[b][:, cols], wg[b][:, cols], MULT)
+            for cols in (whole,):
+                put_plain(pg0[b], idx2, cols, base_t[b][:, cols])
+        r_first = arena.tile([P, S + HALF], F32, name="r_first", offset=11264)
+        recall(0, whole, xr_zero[:])
+        recall(1, halves[0], base2_given[:, halves[0]])
+        for b, g in ((0, 0), (1, 0), (0, 1), (1, 1), (0, 2)):
+            cols = GROUPS[g]
+            xr = (xr_zero, base2_given)[b]
+            make_x(g, (b,), xr[:, cols], r_first[:, S * b :][:, cols], sg_late[:, S * b :][:, cols], [bank[4 + b]])
         weigh(0, 0, 2)
-        make_x(2, (0,), base_t[1][:, halves[1]], r_first[:, 768:], sg_late[:, 1024:1536], [bank[6]])
         xr_two = arena.tile([P, 256], F32, name="xr_two", offset=17920)
-        make_x(0, (2,), xr_two[:], base_t[0][:, quarters[1]], sg_late[:, quarters[2]], [bank[4]])
+        recall(2, GROUPS[0], xr_two[:])
+        make_x(0, (2,), xr_two[:], base_t[0][:, quarters[1]], sg_late[:, 1536:1792], [bank[4]])
         xr_three = arena.tile([P, 256], F32, name="xr_three", offset=17408)
-        make_x(0, (3,), xr_three[:], r_first[:, quarters[2]], sg_late[:, quarters[3]], [bank[5]])
+        recall(3, GROUPS[0], xr_three[:])
+        make_x(0, (3,), xr_three[:], base_t[0][:, quarters[2]], sg_late[:, 1792:2048], [bank[5]])
         weigh(0, 2, 2)
         turn_back(0, [bank[6]], nc.vector.tensor_copy)
         quantise_x(0)
@@ -326,7 +311,7 @@ def tile_list_patch_pulse_page_kernel(
             put_plain(pg1[n], idx4, GROUPS[g], dst)
 
         xr_late = arena.tile([P, 2560], F32, name="xr_late", offset=18432)
-        xr_last = arena.tile([P, HALF], F32, name="xr_last", offset=30720)
+        xr_last = xr_late[:, :HALF]
         r_late = arena.tile([P, 3072], F32, name="r_late", offset=0)
 
         for n in range(BLOCKS):
@@ -334,9 +319,9 @@ def tile_list_patch_pulse_page_kernel(
         pulses_direct(0, 0, bank[0][:, :256], x_of(0, 0))
         pulses_direct(0, 1, bank[1][:, :256], x_of(0, 1))
         pulses_direct(0, 3, bank[3][:, :256], x_of(0, 3))
-        make_x(1, (0,), xr_late[:, 0:256], r_late[:, 0:256], sg_late[:, 0:256], [bank[4], bank[5]])
-        make_x(1, (1,), xr_late[:, 256:512], r_late[:, 256:512], sg_late[:, 256:512], [bank[4], bank[5]][1:])
+        recall(2, GROUPS[1], xr_late[:, 512:768])
         make_x(1, (2,), xr_late[:, 512:768], r_late[:, 512:768], sg_late[:, 512:768], [bank[4], bank[5]])
+        recall(3, GROUPS[1], xr_late[:, 768:1024])
         make_x(1, (3,), xr_late[:, 768:1024], r_late[:, 768:1024], sg_late[:, 768:1024], [bank[4], bank[5]][1:])
         turn_back(1, [bank[7]], nc.scalar.copy)
         quantise_x(1)
@@ -347,9 +332,12 @@ def tile_list_patch_pulse_page_kernel(
         weigh(1, 0, 2)
         pulses_direct(1, 0, bank[0][:, 256:], x_of(1, 0))
         pulses_direct(1, 1, bank[1][:, 256:], x_of(1, 1))
+        recall(1, GROUPS[2], xr_late[:, 1536:2048])
         make_x(2, (1,), xr_late[:, 1536:2048], r_late[:, 1536:2048], sg_late[:, 1536:2048], [bank[5]])
+        recall(2, GROUPS[2], xr_late[:, 2048:2560])
         make_x(2, (2,), xr_late[:, 2048:2560], r_late[:, 2048:2560], sg_late[:, 2048:2560], [bank[4]])
-        make_x(2, (3,), xr_last[:], r_late[:, 2560:], sg_late[:, :HALF], [bank[5]])
+        recall(3, GROUPS[2], xr_last)
+        make_x(2, (3,), xr_last, r_late[:, 2560:], sg_late[:, :HALF], [bank[5]])
         turn_back(2, [bank[6], bank[7]], nc.scalar.copy)
         quantise_x(2)
         y_b = arena.tile([P, 256], F32, name="y_b", offset=30720 + 8 * GROUPS[2].start)

@@ -19,16 +19,36 @@ ADD = mybir.AluOpType.add
 ACT = mybir.ActivationFunctionType
 
 P = 128
-PASSES = K // 512
+PASS_K = 4 * P
+PASSES = K // PASS_K
 BLOCKS = H // P
-HALF = 512
-FIRST = slice(0, 256)
-REST = slice(256, 1024)
-GROUPS = (slice(0, 256), slice(256, 512), slice(512, 1024))
+QUADRANTS = 4
+PER_COLUMN = 16
+BANK = 512
+NARROW = 256
+WHOLE = slice(0, S)
+HALVES = (slice(0, BANK), slice(BANK, S))
+GROUPS = (slice(0, NARROW), slice(NARROW, 2 * NARROW), slice(2 * NARROW, S))
+WIDTHS = tuple(g.stop - g.start for g in GROUPS)
+
+KIB = 1024
+W1_RAW_AT = (0, 6 * KIB, 24 * KIB, 12 * KIB)
+EARLY_RECIP_AT = 9 * KIB
+XR3_FIRST_AT = 17 * KIB
+XR2_FIRST_AT = 17 * KIB + 512
+XR_LATE_AT = 18 * KIB
+BASE3_AT = 19 * KIB
+RECIP3_FIRST_AT = 0
+LATE_RECIP_AT = 0
+X_WOVEN_AT = 30 * KIB
 
 
 def entries(offsets, cols):
-    return offsets[:, cols.start // 16 : cols.stop // 16]
+    return offsets[:, cols.start // PER_COLUMN : cols.stop // PER_COLUMN]
+
+
+def rows(b):
+    return slice(P * b, P * (b + 1))
 
 
 def tile_list_patch_pulse_page_kernel(
@@ -39,319 +59,284 @@ def tile_list_patch_pulse_page_kernel(
     with ExitStack() as ctx:
         lists = ctx.enter_context(tc.tile_pool(name="lists", bufs=1))
         keep = ctx.enter_context(tc.tile_pool(name="keep", bufs=1))
-        arena = ctx.enter_context(tc.tile_pool(name="arena", bufs=1))
+        shared = ctx.enter_context(tc.tile_pool(name="shared", bufs=1))
         psum = ctx.enter_context(tc.psum_pool(name="psum", bufs=1))
 
-        bank = [psum.tile([P, 512], F32, name=f"bank{i}") for i in range(8)]
-        idx1 = lists.tile([P, S // 16], U16, name="idx1")
-        idx2 = lists.tile([P, S // 16], U16, name="idx2")
-        idx3 = lists.tile([P, S // 16], U16, name="idx3")
-        idx4 = lists.tile([P, S // 16], U16, name="idx4")
+        bank = [psum.tile([P, BANK], F32, name=f"bank{i}") for i in range(8)]
+        pick_at = lists.tile([P, S // PER_COLUMN], U16, name="pick_at")
+        patch_at = lists.tile([P, S // PER_COLUMN], U16, name="patch_at")
+        recall_at = lists.tile([P, S // PER_COLUMN], U16, name="recall_at")
+        pulse_at = lists.tile([P, S // PER_COLUMN], U16, name="pulse_at")
 
         tab_w = [keep.tile([P, T], I32, name=f"tab_w{a}") for a in range(PASSES)]
         tab_s = keep.tile([P, T], U8, name="tab_s")
         v_w = [keep.tile([P, S], U32, name=f"v_w{a}", align_bytes=64) for a in range(PASSES)]
         v_s = keep.tile([P, S], U8, name="v_s", align_bytes=64)
-        raw_at = (0, 6144, 18432, 12288)
-        raw = [
-            [arena.tile([P, 4, P], F32, name=f"raw{b}_{a}", offset=raw_at[b] + 2048 * a) for a in range(PASSES)]
+        w1_raw = [
+            [shared.tile([P, 4, P], F32, name=f"w1_raw{b}_{a}", offset=W1_RAW_AT[b] + 2 * KIB * a) for a in range(PASSES)]
             for b in range(BLOCKS)
         ]
-        w1_c = [keep.tile([P, PASSES * P], U32, name=f"w1_c{b}", align_bytes=64) for b in range(BLOCKS)]
+        w1_bf = [keep.tile([P, K], BF16, name=f"w1_bf{b}", align_bytes=64) for b in range(BLOCKS)]
+        w1_w = [keep.tile([P, PASSES * P], U32, name=f"w1_w{b}", align_bytes=64) for b in range(BLOCKS)]
         w1_s = [keep.tile([P, PASSES * P], U8, name=f"w1_s{b}", align_bytes=64) for b in range(BLOCKS)]
-        base_t = [keep.tile([P, S], F32, name=f"base{b}") for b in range(BLOCKS - 1)]
-        base_t.append(arena.tile([P, S], F32, name="base3", offset=24576))
+        state = [keep.tile([P, S], F32, name=f"state{b}") for b in range(BLOCKS - 1)]
+        state.append(shared.tile([P, S], F32, name="state3", offset=BASE3_AT))
+        base2 = keep.tile([P, S], F32, name="base2")
+        base_t = [state[0], state[1], base2, state[3]]
         wgs_t = keep.tile([P, S], F32, name="wgs_t")
-        x = [keep.tile([P, BLOCKS * (g.stop - g.start)], F32, name=f"x{i}") for i, g in enumerate(GROUPS)]
-        wg = [x[0], x[1], x[2][:, :S], x[2][:, S:]]
-        base2_given = keep.tile([P, S], F32, name="base2_given")
-        sg_late = keep.tile([P, 2560], F32, name="sg_late")
-        ebuf = [base_t[1], base_t[2]]
-        pg0 = [keep.tile([P, T], F32, name=f"pg0_{b}") for b in range(BLOCKS)]
-        pg1 = [keep.tile([P, T], F32, name=f"pg1_{b}") for b in range(BLOCKS)]
         wgo_t = keep.tile([P, S], F32, name="wgo_t")
-        x_t = [keep.tile([P, 4 * (g.stop - g.start)], BF16, name=f"x_t{i}") for i, g in enumerate(GROUPS)]
-        x_g = [
-            arena.tile([P, 4 * (g.stop - g.start)], BF16, name=f"x_g{i}", align_bytes=64, offset=30720 + 8 * g.start)
-            for i, g in enumerate(GROUPS)
+        x = [keep.tile([P, BLOCKS * w], F32, name=f"x{g}") for g, w in enumerate(WIDTHS)]
+        weight = [x[0], x[1], x[2][:, S:], keep.tile([P, S], F32, name="weight3")]
+        xr0 = keep.tile([P, S], F32, name="xr0")
+        sign = keep.tile([P, 2 * S + 2 * NARROW], F32, name="sign")
+        pg0 = [keep.tile([P, T], F32, name=f"pg0_{b}") for b in range(BLOCKS)]
+        pg1 = [keep.tile([P, T], F32, name=f"pg1_{n}") for n in range(BLOCKS)]
+        x_turned = [keep.tile([P, 4 * w], BF16, name=f"x_turned{g}") for g, w in enumerate(WIDTHS)]
+        x_woven = [
+            shared.tile([P, 4 * w], BF16, name=f"x_woven{g}", align_bytes=64, offset=X_WOVEN_AT + 8 * GROUPS[g].start)
+            for g, w in enumerate(WIDTHS)
         ]
-        x_c = [keep.tile([P, g.stop - g.start], U32, name=f"x_c{i}", align_bytes=64) for i, g in enumerate(GROUPS)]
-        x_s = [keep.tile([P, g.stop - g.start], U8, name=f"x_s{i}", align_bytes=64) for i, g in enumerate(GROUPS)]
+        x_w = [keep.tile([P, w], U32, name=f"x_w{g}", align_bytes=64) for g, w in enumerate(WIDTHS)]
+        x_s = [keep.tile([P, w], U8, name=f"x_s{g}", align_bytes=64) for g, w in enumerate(WIDTHS)]
         w4_w = keep.tile([P, 2 * H], U8, name="w4_w", align_bytes=64)
         w4_s = keep.tile([P, H], U8, name="w4_s", align_bytes=64)
         ident = keep.tile([P, P], F32, name="ident")
         vec_rows = keep.tile([P, P], F32, name="vec_rows")
         vec_cols = keep.tile([P, 2 * BLOCKS], F32, name="vec_cols")
-        w1_b = [keep.tile([P, PASSES * 512], BF16, name=f"w1_b{b}", align_bytes=64) for b in range(BLOCKS)]
-        xr_zero = keep.tile([P, S], F32, name="xr_zero")
 
         nc.gpsimd.memset(tab_s[:].bitcast(I32), 0)
         nc.vector.memset(w4_s[:].bitcast(I32), 0)
         nc.gpsimd.memset(vec_rows[:], 0.0)
         make_identity(nc, ident[:])
 
-        warm = keep.tile([P, 1], F32, name="warm")
-        nc.scalar.activation(warm[:], ident[:, 0:1], ACT.Abs_reciprocal_sqrt, bias=1.0)
+        def load_table(a):
+            nc.sync.dma_start(tab_w[a][:], tab_words[a].rearrange("p t i -> p (t i)").bitcast(I32))
+
+        def load_scales(tile, source):
+            count = 4 * source.shape[0]
+            for q in range(QUADRANTS):
+                nc.sync.dma_start(tile[32 * q : 32 * q + count, :].bitcast(I32), source[:, 4 * q : 4 * q + 4, :].bitcast(I32))
 
         def load_w1(b):
             for a in range(PASSES):
-                nc.sync.dma_start(raw[b][a][:], w1[512 * a : 512 * (a + 1), P * b : P * (b + 1)].rearrange("(p i) c -> p i c", i=4))
+                k_rows = w1[PASS_K * a : PASS_K * (a + 1), rows(b)]
+                nc.sync.dma_start(w1_raw[b][a][:], k_rows.rearrange("(p t) c -> p t c", t=4))
 
-        def load_tab(a):
-            nc.sync.dma_start(tab_w[a][:], tab_words[a].rearrange("p t i -> p (t i)").bitcast(I32))
+        def load_rows(tiles, source, b):
+            nc.sync.dma_start(tiles[b][:], source[rows(b), :])
 
-        def rows(b):
-            return slice(P * b, P * (b + 1))
-
-        nc.sync.dma_start(idx1[:], offs)
-        load_tab(0)
-        load_tab(1)
-        for q in range(4):
-            nc.sync.dma_start(
-                tab_s[32 * q : 32 * q + 4 * PASSES, :].bitcast(I32), tab_scales[:, 4 * q : 4 * q + 4, :].bitcast(I32)
-            )
+        nc.sync.dma_start(pick_at[:], offs)
+        load_table(0)
+        load_table(1)
+        load_scales(tab_s, tab_scales)
         load_w1(0)
-        load_tab(2)
+        load_table(2)
         nc.sync.dma_start(vec_rows[0:BLOCKS, :], gain.rearrange("(b p) -> b p", p=P))
         nc.sync.dma_start(vec_rows[BLOCKS : 2 * BLOCKS, :], knee.rearrange("(b p) -> b p", p=P))
-        nc.sync.dma_start(idx2[:], offs2)
-        nc.sync.dma_start(wgs_t[:, :HALF], wgs[:, :HALF])
-        nc.sync.dma_start(base_t[0][:], base[rows(0), :])
-        nc.sync.dma_start(pg0[0][:], page0[rows(0), :])
+        nc.sync.dma_start(patch_at[:], offs2)
+        nc.sync.dma_start(wgs_t[:, HALVES[0]], wgs[:, HALVES[0]])
+        load_rows(base_t, base, 0)
+        load_rows(pg0, page0, 0)
         load_w1(1)
-        nc.sync.dma_start(wgs_t[:, HALF:], wgs[:, HALF:])
-        nc.sync.dma_start(base_t[1][:], base[rows(1), :])
+        nc.sync.dma_start(wgs_t[:, HALVES[1]], wgs[:, HALVES[1]])
+        load_rows(base_t, base, 1)
         load_w1(2)
-        nc.sync.dma_start(idx3[:], offs3)
-        nc.sync.dma_start(pg0[1][:], page0[rows(1), :])
+        nc.sync.dma_start(recall_at[:], offs3)
+        load_rows(pg0, page0, 1)
         load_w1(3)
         nc.sync.dma_start(w4_w[:].bitcast(I32), w4_words[0].bitcast(I32))
-        for q in range(4):
-            nc.sync.dma_start(w4_s[32 * q : 32 * q + 4, :].bitcast(I32), w4_scales[0, 4 * q : 4 * q + 4, :].bitcast(I32))
-        nc.sync.dma_start(idx4[:], offs4)
+        load_scales(w4_s, w4_scales)
+        nc.sync.dma_start(pulse_at[:], offs4)
         nc.sync.dma_start(wgo_t[:], wgo)
-        nc.sync.dma_start(base2_given[:], base[rows(2), :])
-        nc.sync.dma_start(base_t[3][:], base[rows(3), :])
-        nc.sync.dma_start(pg0[2][:], page0[rows(2), :])
-        for page, src, n in ((pg1, page1, 0), (pg1, page1, 1), (pg0, page0, 3), (pg1, page1, 3), (pg1, page1, 2)):
-            nc.sync.dma_start(page[n][:], src[rows(n), :])
-
-        def cast_w1(b):
-            for a in range(PASSES):
-                nc.scalar.copy(
-                    w1_b[b][:, 512 * a : 512 * (a + 1)].rearrange("p (c j t) -> p c t j", j=4, t=4),
-                    raw[b][a][:].rearrange("p t (c j) -> p c t j", j=4),
-                )
-
-        def quantise_w1(b):
-            for c0, c1 in ((0, 256), (256, 384)):
-                nc.vector.quantize_mx(w1_c[b][:, c0:c1].bitcast(FP8X4), w1_s[b][:, c0:c1], w1_b[b][:, 4 * c0 : 4 * c1])
-
-        def first_product(b, cols, dst):
-            for a in range(PASSES):
-                nc.tensor.matmul_mx(
-                    dst,
-                    lhsT=w1_c[b][:, P * a : P * (a + 1)].bitcast(FP8X4),
-                    lhsT_scale=w1_s[b][:, P * a : P * (a + 1)],
-                    rhs=v_w[a][:, cols].bitcast(FP8X4),
-                    rhs_scale=v_s[4 * a : P, cols],
-                    start=(a == 0),
-                    stop=(a == PASSES - 1),
-                )
-
-        def scale_wgs(b, cols):
-            nc.scalar.activation(wg[b][:, cols], wgs_t[:, cols], ACT.Copy, scale=vec_cols[:, b : b + 1])
-
-        def evacuate(dst, src):
-            nc.scalar.copy(dst, src)
-
-        def pool_op(dst, a, b, op):
-            nc.gpsimd.tensor_tensor(dst, a, b, op)
-
-        def put_plain(page, idx, cols, values):
-            nc.vector.tensor_copy(page[:].indirect(entries(idx, cols)), values)
-
-        def recall(b, cols, xr):
-            nc.vector.tensor_copy(xr, pg0[b][:].indirect(entries(idx3, cols)))
-
-        def damped(blocks, xr, r, sg, into):
-            width = xr.shape[1] // len(blocks)
-            nc.scalar.activation(r, xr, ACT.Abs)
-            for i, b in enumerate(blocks):
-                cols = slice(width * i, width * (i + 1))
-                knee_b = vec_cols[:, BLOCKS + b : BLOCKS + b + 1]
-                nc.scalar.activation(sg[:, cols], r[:, cols], ACT.Sign, bias=1.0, scale=knee_b)
-                nc.scalar.activation(r[:, cols], r[:, cols], ACT.Abs_reciprocal_sqrt, bias=1.0, scale=knee_b)
-            nc.scalar.activation(r, r, ACT.Square)
-            pool_op(xr, xr, sg, MULT)
-            pool_op(into, xr, r, MULT)
-
-        def turn(b, g, x, dst):
-            tiles = (GROUPS[g].stop - GROUPS[g].start) // P
-            for j in range(tiles):
-                nc.tensor.transpose(dst[:, P * j : P * (j + 1)], x[:, P * j : P * (j + 1)], ident[:])
-            nc.scalar.copy(
-                x_t[g][:].rearrange("p (j u q e) -> p j u q e", u=2, q=P, e=2)[:, :, :, 32 * b : 32 * (b + 1), :],
-                dst[:, : P * tiles].rearrange("p (j q u e) -> p j u q e", q=32, u=2, e=2),
-            )
-
-        def turn_back(g, dsts, copy):
-            words = x_t[g][:].bitcast(F32)
-            woven = x_g[g][:].bitcast(F32)
-            for i, dst in enumerate(dsts):
-                for s in range(4):
-                    nc.tensor.transpose(dst[:, P * s : P * (s + 1)], words[:, 512 * i + P * s : 512 * i + P * (s + 1)], ident[:])
-                copy(
-                    woven[:, 512 * i : 512 * (i + 1)].rearrange("p (j m u) -> p j m u", j=2, u=2),
-                    dst[:].rearrange("p (j u m) -> p j m u", j=2, u=2),
-                )
-
-        def quantise_x(g):
-            nc.vector.quantize_mx(x_c[g][:].bitcast(FP8X4), x_s[g][:], x_g[g][:])
-
-        def second_product(n, g, dst):
-            nc.tensor.matmul_mx(
-                dst,
-                lhsT=w4_w[:, 2 * P * n : 2 * P * (n + 1)].bitcast(FP4X4),
-                lhsT_scale=w4_s[:, rows(n)],
-                rhs=x_c[g][:].bitcast(FP8X4),
-                rhs_scale=x_s[g][:],
-                start=True,
-                stop=True,
-            )
-
-        halves = (slice(0, HALF), slice(HALF, S))
-        quarters = [slice(256 * i, 256 * (i + 1)) for i in range(4)]
-
-        whole = slice(0, S)
+        load_rows(pg1, page1, 0)
+        load_rows(base_t, base, 2)
+        load_rows(base_t, base, 3)
+        load_rows(pg0, page0, 2)
+        load_rows(pg1, page1, 1)
+        load_rows(pg0, page0, 3)
+        load_rows(pg1, page1, 3)
+        load_rows(pg1, page1, 2)
 
         def pick(a, cols):
-            nc.vector.tensor_copy(v_w[a][:, cols], tab_w[a][:].bitcast(U32).indirect(entries(idx1, cols)))
+            nc.vector.tensor_copy(v_w[a][:, cols], tab_w[a][:].bitcast(U32).indirect(entries(pick_at, cols)))
 
-        def add_base(b, given):
-            for h, cols in enumerate(halves):
-                first_product(b, cols, bank[2 * (b % 2) + h][:])
-                nc.vector.tensor_tensor(base_t[b][:, cols], bank[2 * (b % 2) + h][:], given[:, cols], ADD)
+        def quantise_w1(b):
+            for a in range(PASSES):
+                nc.scalar.copy(
+                    w1_bf[b][:, PASS_K * a : PASS_K * (a + 1)].rearrange("p (c j t) -> p c t j", j=4, t=4),
+                    w1_raw[b][a][:].rearrange("p t (c j) -> p c t j", j=4),
+                )
+            for c0, c1 in ((0, 2 * P), (2 * P, 3 * P)):
+                nc.vector.quantize_mx(w1_w[b][:, c0:c1].bitcast(FP8X4), w1_s[b][:, c0:c1], w1_bf[b][:, 4 * c0 : 4 * c1])
+
+        def add_product(b):
+            for h, cols in enumerate(HALVES):
+                sums = bank[2 * (b % 2) + h][:]
+                for a in range(PASSES):
+                    nc.tensor.matmul_mx(
+                        sums,
+                        lhsT=w1_w[b][:, rows(a)].bitcast(FP8X4),
+                        lhsT_scale=w1_s[b][:, rows(a)],
+                        rhs=v_w[a][:, cols].bitcast(FP8X4),
+                        rhs_scale=v_s[4 * a : P, cols],
+                        start=(a == 0),
+                        stop=(a == PASSES - 1),
+                    )
+                nc.vector.tensor_tensor(state[b][:, cols], sums, base_t[b][:, cols], ADD)
+
+        def make_weight(b, cols):
+            nc.scalar.activation(weight[b][:, cols], wgs_t[:, cols], ACT.Copy, scale=vec_cols[:, b : b + 1])
+
+        def patch(b):
+            add_product(b)
+            for cols in HALVES:
+                nc.gpsimd.tensor_tensor(state[b][:, cols], state[b][:, cols], weight[b][:, cols], MULT)
+            nc.vector.tensor_copy(pg0[b][:].indirect(patch_at[:]), state[b][:])
+
+        def recall(b, cols, xr):
+            nc.vector.tensor_copy(xr, pg0[b][:].indirect(entries(recall_at, cols)))
 
         def x_of(g, b, count=1):
-            width = GROUPS[g].stop - GROUPS[g].start
-            return x[g][:, width * b : width * (b + count)]
+            return x[g][:, WIDTHS[g] * b : WIDTHS[g] * (b + count)]
 
-        def weigh(g, b, count=1, src=None):
-            width = GROUPS[g].stop - GROUPS[g].start
-            src = x_of(g, b, count) if src is None else src
-            nc.gpsimd.tensor_tensor(
-                x_of(g, b, count).rearrange("p (n c) -> p n c", n=count),
-                src.rearrange("p (n c) -> p n c", n=count),
-                wgo_t[:, GROUPS[g]].unsqueeze(1).to_broadcast([P, count, width]),
-                MULT,
+        def damp(g, b, xr, recip, sgn, via):
+            knee_b = vec_cols[:, BLOCKS + b : BLOCKS + b + 1]
+            nc.scalar.activation(recip, xr, ACT.Abs)
+            nc.scalar.activation(sgn, recip, ACT.Sign, bias=1.0, scale=knee_b)
+            nc.scalar.activation(recip, recip, ACT.Abs_reciprocal_sqrt, bias=1.0, scale=knee_b)
+            nc.scalar.activation(recip, recip, ACT.Square)
+            nc.gpsimd.tensor_tensor(xr, xr, sgn, MULT)
+            nc.gpsimd.tensor_tensor(x_of(g, b), xr, recip, MULT)
+            for j in range(WIDTHS[g] // P):
+                nc.tensor.transpose(via[:, rows(j)], x_of(g, b)[:, rows(j)], ident[:])
+            nc.scalar.copy(
+                x_turned[g][:].rearrange("p (j u q e) -> p j u q e", u=2, q=P, e=2)[:, :, :, 32 * b : 32 * (b + 1), :],
+                via[:, : WIDTHS[g]].rearrange("p (j q u e) -> p j u q e", q=32, u=2, e=2),
             )
 
-        def make_x(g, blocks, xr, r, sg, banks, into=None):
-            width = GROUPS[g].stop - GROUPS[g].start
-            into = x_of(g, blocks[0], len(blocks)) if into is None else into
-            damped(blocks, xr, r, sg, into)
-            for i, b in enumerate(blocks):
-                turn(b, g, into[:, width * i : width * (i + 1)], banks[i])
+        def quantise_x(g, banks, copy):
+            pairs = x_turned[g][:].bitcast(F32)
+            woven = x_woven[g][:].bitcast(F32)
+            for i, via in enumerate(banks):
+                piece = slice(BANK * i, BANK * (i + 1))
+                for j in range(BANK // P):
+                    nc.tensor.transpose(via[:, rows(j)], pairs[:, piece][:, rows(j)], ident[:])
+                copy(
+                    woven[:, piece].rearrange("p (j m u) -> p j m u", j=2, u=2),
+                    via[:].rearrange("p (j u m) -> p j m u", j=2, u=2),
+                )
+            nc.vector.quantize_mx(x_w[g][:].bitcast(FP8X4), x_s[g][:], x_woven[g][:])
 
-        pick(0, whole)
-        pick(1, whole)
-        nc.vector.tensor_copy(v_s[:], tab_s[:].indirect(idx1[:]))
-        cast_w1(0)
+        def weigh(g, b, count):
+            blocks = x_of(g, b, count).rearrange("p (n c) -> p n c", n=count)
+            nc.gpsimd.tensor_tensor(blocks, blocks, wgo_t[:, GROUPS[g]].unsqueeze(1).to_broadcast([P, count, WIDTHS[g]]), MULT)
+
+        def second_product(g, sums):
+            for n in range(BLOCKS):
+                nc.tensor.matmul_mx(
+                    sums[n],
+                    lhsT=w4_w[:, 2 * P * n : 2 * P * (n + 1)].bitcast(FP4X4),
+                    lhsT_scale=w4_s[:, rows(n)],
+                    rhs=x_w[g][:].bitcast(FP8X4),
+                    rhs_scale=x_s[g][:],
+                    start=True,
+                    stop=True,
+                )
+
+        def scatter_pulse(g, n, values):
+            nc.vector.tensor_copy(pg1[n][:].indirect(entries(pulse_at, GROUPS[g])), values)
+
+        def pulse(g, n, sums, values):
+            nc.vector.tensor_tensor(values, sums, x_of(g, n), MULT)
+            scatter_pulse(g, n, values)
+
+        pick(0, WHOLE)
+        pick(1, WHOLE)
+        nc.vector.tensor_copy(v_s[:], tab_s[:].indirect(pick_at[:]))
         quantise_w1(0)
-        for cols in halves:
+        for cols in HALVES:
             pick(2, cols)
         nc.tensor.transpose(bank[4][:, :P], vec_rows[:], ident[:])
         nc.scalar.copy(vec_cols[:], bank[4][:, : 2 * BLOCKS])
-        add_base(0, base_t[0])
-        cast_w1(1)
+
+        add_product(0)
         quantise_w1(1)
-        for cols in halves:
-            scale_wgs(0, cols)
-            nc.vector.tensor_tensor(pg0[0][:].indirect(entries(idx2, cols)), base_t[0][:, cols], wg[0][:, cols], MULT)
-        for b in (1, 2, 3):
-            scale_wgs(b, whole)
-        for b in (2, 3):
-            cast_w1(b)
-            quantise_w1(b)
-        for b in (1, 2, 3):
-            add_base(b, base2_given if b == 2 else base_t[b])
-            for cols in halves:
-                pool_op(base_t[b][:, cols], base_t[b][:, cols], wg[b][:, cols], MULT)
-            for cols in (whole,):
-                put_plain(pg0[b], idx2, cols, base_t[b][:, cols])
-        r_first = arena.tile([P, S + HALF], F32, name="r_first", offset=11264)
-        recall(0, whole, xr_zero[:])
-        recall(1, halves[0], base2_given[:, halves[0]])
-        for b, g in ((0, 0), (1, 0), (0, 1), (1, 1), (0, 2)):
-            cols = GROUPS[g]
-            xr = (xr_zero, base2_given)[b]
-            make_x(g, (b,), xr[:, cols], r_first[:, S * b :][:, cols], sg_late[:, S * b :][:, cols], [bank[4 + b]])
+        for cols in HALVES:
+            make_weight(0, cols)
+            nc.vector.tensor_tensor(pg0[0][:].indirect(entries(patch_at, cols)), state[0][:, cols], weight[0][:, cols], MULT)
+        for b in range(1, BLOCKS):
+            make_weight(b, WHOLE)
+        quantise_w1(2)
+        quantise_w1(3)
+        patch(1)
+        patch(2)
+
+        early_recip = shared.tile([P, 2 * S], F32, name="early_recip", offset=EARLY_RECIP_AT)
+
+        def damp_early(b, g, via):
+            cols = slice(S * b + GROUPS[g].start, S * b + GROUPS[g].stop)
+            damp(g, b, (xr0, base2)[b][:, GROUPS[g]], early_recip[:, cols], sign[:, cols], via)
+
+        recall(0, WHOLE, xr0[:])
+        for g in range(len(GROUPS)):
+            damp_early(0, g, bank[2 + g])
+        patch(3)
+        recall(1, WHOLE, base2[:])
+        damp_early(1, 0, bank[5])
+        damp_early(1, 1, bank[4])
         weigh(0, 0, 2)
-        xr_two = arena.tile([P, 256], F32, name="xr_two", offset=17920)
-        recall(2, GROUPS[0], xr_two[:])
-        make_x(0, (2,), xr_two[:], base_t[0][:, quarters[1]], sg_late[:, 1536:1792], [bank[4]])
-        xr_three = arena.tile([P, 256], F32, name="xr_three", offset=17408)
-        recall(3, GROUPS[0], xr_three[:])
-        make_x(0, (3,), xr_three[:], base_t[0][:, quarters[2]], sg_late[:, 1792:2048], [bank[5]])
+        xr2_first = shared.tile([P, NARROW], F32, name="xr2_first", offset=XR2_FIRST_AT)
+        recall(2, GROUPS[0], xr2_first[:])
+        damp(0, 2, xr2_first[:], state[0][:, :NARROW], sign[:, 2 * S : 2 * S + NARROW], bank[4])
+        damp_early(1, 2, bank[5])
+
+        xr3_first = shared.tile([P, NARROW], F32, name="xr3_first", offset=XR3_FIRST_AT)
+        recip3_first = shared.tile([P, NARROW], F32, name="recip3_first", offset=RECIP3_FIRST_AT)
+        recall(3, GROUPS[0], xr3_first[:])
+        damp(0, 3, xr3_first[:], recip3_first[:], sign[:, 2 * S + NARROW :], bank[5])
         weigh(0, 2, 2)
-        turn_back(0, [bank[6]], nc.vector.tensor_copy)
-        quantise_x(0)
+        quantise_x(0, [bank[6]], nc.vector.tensor_copy)
 
-        def pulses(g, n, src, count=1):
-            width = GROUPS[g].stop - GROUPS[g].start
-            staged = ebuf[n % 2][:, GROUPS[g].start : GROUPS[g].start + width * count]
-            evacuate(staged, src)
-            pool_op(x_of(g, n, count), staged, x_of(g, n, count), MULT)
-            for m in range(n, n + count):
-                put_plain(pg1[m], idx4, GROUPS[g], x_of(g, m))
+        late_width = 2 * (WIDTHS[1] + WIDTHS[2])
+        xr_late = shared.tile([P, late_width], F32, name="xr_late", offset=XR_LATE_AT)
+        late_recip = shared.tile([P, late_width], F32, name="late_recip", offset=LATE_RECIP_AT)
 
-        def pulses_direct(g, n, src, dst):
-            nc.vector.tensor_tensor(dst, src, x_of(g, n), MULT)
-            put_plain(pg1[n], idx4, GROUPS[g], dst)
+        def damp_late(g, banks):
+            for i, via in enumerate(banks):
+                start = 2 * sum(WIDTHS[1:g]) + i * WIDTHS[g]
+                cols = slice(start, start + WIDTHS[g])
+                recall(2 + i, GROUPS[g], xr_late[:, cols])
+                damp(g, 2 + i, xr_late[:, cols], late_recip[:, cols], sign[:, cols], via)
 
-        xr_late = arena.tile([P, 2560], F32, name="xr_late", offset=18432)
-        xr_last = xr_late[:, :HALF]
-        r_late = arena.tile([P, 3072], F32, name="r_late", offset=0)
+        def after_quantise(g, width):
+            return shared.tile([P, width], F32, name=f"after_quantise{g}", offset=X_WOVEN_AT + 8 * GROUPS[g].start)
 
-        for n in range(BLOCKS):
-            second_product(n, 0, bank[n][:, :256])
-        pulses_direct(0, 0, bank[0][:, :256], x_of(0, 0))
-        pulses_direct(0, 1, bank[1][:, :256], x_of(0, 1))
-        pulses_direct(0, 3, bank[3][:, :256], x_of(0, 3))
-        recall(2, GROUPS[1], xr_late[:, 512:768])
-        make_x(1, (2,), xr_late[:, 512:768], r_late[:, 512:768], sg_late[:, 512:768], [bank[4], bank[5]])
-        recall(3, GROUPS[1], xr_late[:, 768:1024])
-        make_x(1, (3,), xr_late[:, 768:1024], r_late[:, 768:1024], sg_late[:, 768:1024], [bank[4], bank[5]][1:])
-        turn_back(1, [bank[7]], nc.scalar.copy)
-        quantise_x(1)
-        y_a = arena.tile([P, 256], F32, name="y_a", offset=30720 + 8 * GROUPS[1].start)
-        pulses_direct(0, 2, bank[2][:, :256], y_a[:])
-        for n in range(BLOCKS):
-            second_product(n, 1, bank[n][:, 256:])
+        sums0 = [bank[n][:, :NARROW] for n in range(BLOCKS)]
+        second_product(0, sums0)
+        for n in (0, 1, 3):
+            pulse(0, n, sums0[n], x_of(0, n))
+        damp_late(1, (bank[4], bank[0]))
+        quantise_x(1, [bank[7]], nc.scalar.copy)
+        pulse(0, 2, sums0[2], after_quantise(1, NARROW)[:])
+
+        sums1 = [bank[n][:, NARROW:] for n in range(BLOCKS)]
+        second_product(1, sums1)
         weigh(1, 0, 2)
-        pulses_direct(1, 0, bank[0][:, 256:], x_of(1, 0))
-        pulses_direct(1, 1, bank[1][:, 256:], x_of(1, 1))
-        recall(1, GROUPS[2], xr_late[:, 1536:2048])
-        make_x(2, (1,), xr_late[:, 1536:2048], r_late[:, 1536:2048], sg_late[:, 1536:2048], [bank[5]])
-        recall(2, GROUPS[2], xr_late[:, 2048:2560])
-        make_x(2, (2,), xr_late[:, 2048:2560], r_late[:, 2048:2560], sg_late[:, 2048:2560], [bank[4]])
-        recall(3, GROUPS[2], xr_last)
-        make_x(2, (3,), xr_last, r_late[:, 2560:], sg_late[:, :HALF], [bank[5]])
-        turn_back(2, [bank[6], bank[7]], nc.scalar.copy)
-        quantise_x(2)
-        y_b = arena.tile([P, 256], F32, name="y_b", offset=30720 + 8 * GROUPS[2].start)
+        for n in (0, 1):
+            pulse(1, n, sums1[n], x_of(1, n))
+        damp_late(2, (bank[4], bank[5]))
+        quantise_x(2, [bank[6], bank[7]], nc.scalar.copy)
+        held = after_quantise(2, 2 * NARROW)
         weigh(1, 2, 2)
-        pulses_direct(1, 2, bank[2][:, 256:], y_b[:])
-        pulses_direct(1, 3, bank[3][:, 256:], x_of(1, 3))
-        weigh(2, 0, 4)
+        for n in (2, 3):
+            pulse(1, n, sums1[n], held[:, NARROW * (n - 2) : NARROW * (n - 1)])
+
+        weigh(2, 0, BLOCKS)
+        sums2 = [bank[i][:] for i in (0, 1, 4, 5)]
+        second_product(2, sums2)
         for n in range(BLOCKS):
-            second_product(n, 2, bank[(0, 1, 4, 5)[n]][:])
-        pulses(2, 0, bank[0][:])
-        nc.sync.dma_start(out[rows(0), :], pg1[0][:])
-        pulses(2, 1, bank[1][:])
-        nc.sync.dma_start(out[rows(1), :], pg1[1][:])
-        pulses(2, 2, bank[4][:])
-        nc.sync.dma_start(out[rows(2), :], pg1[2][:])
-        pulses(2, 3, bank[5][:])
-        nc.sync.dma_start(out[rows(3), :], pg1[3][:])
+            staged = state[1 + n % 2][:, GROUPS[2]]
+            nc.scalar.copy(staged, sums2[n])
+            nc.gpsimd.tensor_tensor(x_of(2, n), staged, x_of(2, n), MULT)
+            scatter_pulse(2, n, x_of(2, n))
+            nc.sync.dma_start(out[rows(n), :], pg1[n][:])

@@ -32,12 +32,12 @@ GROUPS = (slice(0, NARROW), slice(NARROW, 2 * NARROW), slice(2 * NARROW, S))
 WIDTHS = tuple(g.stop - g.start for g in GROUPS)
 
 KIB = 1024
-W1_RAW_AT = (0, 6 * KIB, 24 * KIB, 12 * KIB)
-EARLY_RECIP_AT = 9 * KIB
+W1_RAW_AT = (0, 6 * KIB, 18 * KIB, 12 * KIB)
+EARLY_RECIP_AT = 11 * KIB
 XR3_FIRST_AT = 17 * KIB
-XR2_FIRST_AT = 17 * KIB + 512
+XR2_FIRST_AT = XR3_FIRST_AT + KIB // 2
 XR_LATE_AT = 18 * KIB
-BASE3_AT = 19 * KIB
+STATE3_AT = 24 * KIB
 RECIP3_FIRST_AT = 0
 LATE_RECIP_AT = 0
 X_WOVEN_AT = 30 * KIB
@@ -80,15 +80,15 @@ def tile_list_patch_pulse_page_kernel(
         w1_w = [keep.tile([P, PASSES * P], U32, name=f"w1_w{b}", align_bytes=64) for b in range(BLOCKS)]
         w1_s = [keep.tile([P, PASSES * P], U8, name=f"w1_s{b}", align_bytes=64) for b in range(BLOCKS)]
         state = [keep.tile([P, S], F32, name=f"state{b}") for b in range(BLOCKS - 1)]
-        state.append(shared.tile([P, S], F32, name="state3", offset=BASE3_AT))
+        state.append(shared.tile([P, S], F32, name="state3", offset=STATE3_AT))
         base2 = keep.tile([P, S], F32, name="base2")
         base_t = [state[0], state[1], base2, state[3]]
         wgs_t = keep.tile([P, S], F32, name="wgs_t")
         wgo_t = keep.tile([P, S], F32, name="wgo_t")
         x = [keep.tile([P, BLOCKS * w], F32, name=f"x{g}") for g, w in enumerate(WIDTHS)]
-        weight = [x[0], x[1], x[2][:, S:], keep.tile([P, S], F32, name="weight3")]
+        weight = [x[0], x[1], x[2][:, :S], x[2][:, S:]]
         xr0 = keep.tile([P, S], F32, name="xr0")
-        sign = keep.tile([P, 2 * S + 2 * NARROW], F32, name="sign")
+        sign = keep.tile([P, 2 * S], F32, name="sign")
         pg0 = [keep.tile([P, T], F32, name=f"pg0_{b}") for b in range(BLOCKS)]
         pg1 = [keep.tile([P, T], F32, name=f"pg1_{n}") for n in range(BLOCKS)]
         x_turned = [keep.tile([P, 4 * w], BF16, name=f"x_turned{g}") for g, w in enumerate(WIDTHS)]
@@ -148,10 +148,10 @@ def tile_list_patch_pulse_page_kernel(
         load_scales(w4_s, w4_scales)
         nc.sync.dma_start(pulse_at[:], offs4)
         nc.sync.dma_start(wgo_t[:], wgo)
-        load_rows(pg1, page1, 0)
         load_rows(base_t, base, 2)
         load_rows(base_t, base, 3)
         load_rows(pg0, page0, 2)
+        load_rows(pg1, page1, 0)
         load_rows(pg1, page1, 1)
         load_rows(pg0, page0, 3)
         load_rows(pg1, page1, 3)
@@ -268,48 +268,38 @@ def tile_list_patch_pulse_page_kernel(
             make_weight(b, WHOLE)
         quantise_w1(2)
         quantise_w1(3)
-        patch(1)
-        patch(2)
+        for b in range(1, BLOCKS):
+            patch(b)
 
-        early_recip = shared.tile([P, 2 * S], F32, name="early_recip", offset=EARLY_RECIP_AT)
-
-        def damp_early(b, g, via):
-            cols = slice(S * b + GROUPS[g].start, S * b + GROUPS[g].stop)
-            damp(g, b, (xr0, base2)[b][:, GROUPS[g]], early_recip[:, cols], sign[:, cols], via)
-
+        early_recip = shared.tile([P, S + 2 * NARROW], F32, name="early_recip", offset=EARLY_RECIP_AT)
         recall(0, WHOLE, xr0[:])
-        for g in range(len(GROUPS)):
-            damp_early(0, g, bank[2 + g])
-        patch(3)
-        recall(1, WHOLE, base2[:])
-        damp_early(1, 0, bank[5])
-        damp_early(1, 1, bank[4])
-        weigh(0, 0, 2)
+        recall(1, HALVES[0], base2[:, HALVES[0]])
+        for g, b in ((0, 0), (0, 1), (1, 0), (1, 1), (2, 0)):
+            cols = slice(S * b + GROUPS[g].start, S * b + GROUPS[g].stop)
+            damp(g, b, (xr0, base2)[b][:, GROUPS[g]], early_recip[:, cols], sign[:, cols], bank[4 + b])
         xr2_first = shared.tile([P, NARROW], F32, name="xr2_first", offset=XR2_FIRST_AT)
         recall(2, GROUPS[0], xr2_first[:])
-        damp(0, 2, xr2_first[:], state[0][:, :NARROW], sign[:, 2 * S : 2 * S + NARROW], bank[4])
-        damp_early(1, 2, bank[5])
+        damp(0, 2, xr2_first[:], state[0][:, :NARROW], sign[:, 2 * S - 2 * NARROW : 2 * S - NARROW], bank[4])
+        weigh(0, 0, 3)
 
         xr3_first = shared.tile([P, NARROW], F32, name="xr3_first", offset=XR3_FIRST_AT)
         recip3_first = shared.tile([P, NARROW], F32, name="recip3_first", offset=RECIP3_FIRST_AT)
         recall(3, GROUPS[0], xr3_first[:])
-        damp(0, 3, xr3_first[:], recip3_first[:], sign[:, 2 * S + NARROW :], bank[5])
-        weigh(0, 2, 2)
+        damp(0, 3, xr3_first[:], recip3_first[:], sign[:, 2 * S - NARROW :], bank[5])
+        weigh(0, 3, 1)
         quantise_x(0, [bank[6]], nc.vector.tensor_copy)
 
-        late_width = 2 * (WIDTHS[1] + WIDTHS[2])
+        late_width = 2 * WIDTHS[1] + 3 * WIDTHS[2]
         xr_late = shared.tile([P, late_width], F32, name="xr_late", offset=XR_LATE_AT)
         late_recip = shared.tile([P, late_width], F32, name="late_recip", offset=LATE_RECIP_AT)
 
         def damp_late(g, banks):
             for i, via in enumerate(banks):
+                b = BLOCKS - len(banks) + i
                 start = 2 * sum(WIDTHS[1:g]) + i * WIDTHS[g]
                 cols = slice(start, start + WIDTHS[g])
-                recall(2 + i, GROUPS[g], xr_late[:, cols])
-                damp(g, 2 + i, xr_late[:, cols], late_recip[:, cols], sign[:, cols], via)
-
-        def after_quantise(g, width):
-            return shared.tile([P, width], F32, name=f"after_quantise{g}", offset=X_WOVEN_AT + 8 * GROUPS[g].start)
+                recall(b, GROUPS[g], xr_late[:, cols])
+                damp(g, b, xr_late[:, cols], late_recip[:, cols], sign[:, cols], via)
 
         sums0 = [bank[n][:, :NARROW] for n in range(BLOCKS)]
         second_product(0, sums0)
@@ -317,26 +307,27 @@ def tile_list_patch_pulse_page_kernel(
             pulse(0, n, sums0[n], x_of(0, n))
         damp_late(1, (bank[4], bank[0]))
         quantise_x(1, [bank[7]], nc.scalar.copy)
-        pulse(0, 2, sums0[2], after_quantise(1, NARROW)[:])
+        held = shared.tile([P, NARROW], F32, name="held", offset=X_WOVEN_AT + 8 * GROUPS[1].start)
+        pulse(0, 2, sums0[2], held[:])
 
         sums1 = [bank[n][:, NARROW:] for n in range(BLOCKS)]
         second_product(1, sums1)
-        weigh(1, 0, 2)
-        for n in (0, 1):
+        for n in range(BLOCKS):
+            if n % 2 == 0:
+                weigh(1, n, 2)
             pulse(1, n, sums1[n], x_of(1, n))
-        damp_late(2, (bank[4], bank[5]))
+        damp_late(2, (bank[5], bank[4], bank[5]))
         quantise_x(2, [bank[6], bank[7]], nc.scalar.copy)
-        held = after_quantise(2, 2 * NARROW)
-        weigh(1, 2, 2)
-        for n in (2, 3):
-            pulse(1, n, sums1[n], held[:, NARROW * (n - 2) : NARROW * (n - 1)])
 
         weigh(2, 0, BLOCKS)
         sums2 = [bank[i][:] for i in (0, 1, 4, 5)]
         second_product(2, sums2)
         for n in range(BLOCKS):
-            staged = state[1 + n % 2][:, GROUPS[2]]
-            nc.scalar.copy(staged, sums2[n])
-            nc.gpsimd.tensor_tensor(x_of(2, n), staged, x_of(2, n), MULT)
-            scatter_pulse(2, n, x_of(2, n))
+            if n == 0:
+                pulse(2, n, sums2[n], x_of(2, n))
+            else:
+                staged = state[1 + n % 2][:, GROUPS[2]]
+                nc.scalar.copy(staged, sums2[n])
+                nc.gpsimd.tensor_tensor(x_of(2, n), staged, x_of(2, n), MULT)
+                scatter_pulse(2, n, x_of(2, n))
             nc.sync.dma_start(out[rows(n), :], pg1[n][:])

from contextlib import ExitStack

import concourse.mybir as mybir
from concourse.masks import make_identity

K, H, T, S = 1536, 512, 2048, 1024
FLOPS = 2 * K * H * S + 2 * H * H * S

F32 = mybir.dt.float32
BF16 = mybir.dt.bfloat16
I32 = mybir.dt.int32
U32 = mybir.dt.uint32
U16 = mybir.dt.uint16
U8 = mybir.dt.uint8
FP8X4 = mybir.dt.float8_e4m3fn_x4
FP4X4 = mybir.dt.float4_e2m1fn_x4
MULT = mybir.AluOpType.mult
ADD = mybir.AluOpType.add
ACT = mybir.ActivationFunctionType

P = 128
PASS_K = 4 * P
PASSES = K // PASS_K
BLOCKS = H // P
QUADRANTS = 4
PER_COLUMN = 16
BANK = 512
NARROW = 256
WHOLE = slice(0, S)
HALVES = (slice(0, BANK), slice(BANK, S))
GROUPS = (slice(0, NARROW), slice(NARROW, 2 * NARROW), slice(2 * NARROW, S))
WIDTHS = tuple(g.stop - g.start for g in GROUPS)

KIB = 1024
W1_RAW_AT = (0, 6 * KIB, 18 * KIB, 12 * KIB)
EARLY_RECIP_AT = 11 * KIB
XR3_FIRST_AT = 17 * KIB
XR2_FIRST_AT = XR3_FIRST_AT + KIB // 2
XR_LATE_AT = 18 * KIB
STATE3_AT = 24 * KIB
RECIP3_FIRST_AT = 0
LATE_RECIP_AT = 0
X_WOVEN_AT = 30 * KIB


def entries(offsets, cols):
    return offsets[:, cols.start // PER_COLUMN : cols.stop // PER_COLUMN]


def rows(b):
    return slice(P * b, P * (b + 1))


def tile_list_patch_pulse_page_kernel(
    tc, tab_words, tab_scales, offs, w1, base, gain, wgs, page0, offs2, offs3, knee,
    w4_words, w4_scales, wgo, page1, offs4, out,
):
    nc = tc.nc
    with ExitStack() as ctx:
        lists = ctx.enter_context(tc.tile_pool(name="lists", bufs=1))
        keep = ctx.enter_context(tc.tile_pool(name="keep", bufs=1))
        shared = ctx.enter_context(tc.tile_pool(name="shared", bufs=1))
        psum = ctx.enter_context(tc.psum_pool(name="psum", bufs=1))

        bank = [psum.tile([P, BANK], F32, name=f"bank{i}") for i in range(8)]
        pick_at = lists.tile([P, S // PER_COLUMN], U16, name="pick_at")
        patch_at = lists.tile([P, S // PER_COLUMN], U16, name="patch_at")
        recall_at = lists.tile([P, S // PER_COLUMN], U16, name="recall_at")
        pulse_at = lists.tile([P, S // PER_COLUMN], U16, name="pulse_at")

        tab_w = [keep.tile([P, T], I32, name=f"tab_w{a}") for a in range(PASSES)]
        tab_s = keep.tile([P, T], U8, name="tab_s")
        v_w = [keep.tile([P, S], U32, name=f"v_w{a}", align_bytes=64) for a in range(PASSES)]
        v_s = keep.tile([P, S], U8, name="v_s", align_bytes=64)
        w1_raw = [
            [shared.tile([P, 4, P], F32, name=f"w1_raw{b}_{a}", offset=W1_RAW_AT[b] + 2 * KIB * a) for a in range(PASSES)]
            for b in range(BLOCKS)
        ]
        w1_bf = [keep.tile([P, K], BF16, name=f"w1_bf{b}", align_bytes=64) for b in range(BLOCKS)]
        w1_w = [keep.tile([P, PASSES * P], U32, name=f"w1_w{b}", align_bytes=64) for b in range(BLOCKS)]
        w1_s = [keep.tile([P, PASSES * P], U8, name=f"w1_s{b}", align_bytes=64) for b in range(BLOCKS)]
        state = [keep.tile([P, S], F32, name=f"state{b}") for b in range(BLOCKS - 1)]
        state.append(shared.tile([P, S], F32, name="state3", offset=STATE3_AT))
        base2 = keep.tile([P, S], F32, name="base2")
        base_t = [state[0], state[1], base2, state[3]]
        wgs_t = keep.tile([P, S], F32, name="wgs_t")
        wgo_t = keep.tile([P, S], F32, name="wgo_t")
        x = [keep.tile([P, BLOCKS * w], F32, name=f"x{g}") for g, w in enumerate(WIDTHS)]
        weight = [x[0], x[1], x[2][:, :S], x[2][:, S:]]
        xr0 = keep.tile([P, S], F32, name="xr0")
        sign = keep.tile([P, 2 * S], F32, name="sign")
        pg0 = [keep.tile([P, T], F32, name=f"pg0_{b}") for b in range(BLOCKS)]
        pg1 = [keep.tile([P, T], F32, name=f"pg1_{n}") for n in range(BLOCKS)]
        x_turned = [keep.tile([P, 4 * w], BF16, name=f"x_turned{g}") for g, w in enumerate(WIDTHS)]
        x_woven = [
            shared.tile([P, 4 * w], BF16, name=f"x_woven{g}", align_bytes=64, offset=X_WOVEN_AT + 8 * GROUPS[g].start)
            for g, w in enumerate(WIDTHS)
        ]
        x_w = [keep.tile([P, w], U32, name=f"x_w{g}", align_bytes=64) for g, w in enumerate(WIDTHS)]
        x_s = [keep.tile([P, w], U8, name=f"x_s{g}", align_bytes=64) for g, w in enumerate(WIDTHS)]
        w4_w = keep.tile([P, 2 * H], U8, name="w4_w", align_bytes=64)
        w4_s = keep.tile([P, H], U8, name="w4_s", align_bytes=64)
        ident = keep.tile([P, P], F32, name="ident")
        vec_rows = keep.tile([P, P], F32, name="vec_rows")
        vec_cols = keep.tile([P, 2 * BLOCKS], F32, name="vec_cols")

        nc.gpsimd.memset(tab_s[:].bitcast(I32), 0)
        nc.vector.memset(w4_s[:].bitcast(I32), 0)
        nc.gpsimd.memset(vec_rows[:], 0.0)
        make_identity(nc, ident[:])

        def load_table(a):
            nc.sync.dma_start(tab_w[a][:], tab_words[a].rearrange("p t i -> p (t i)").bitcast(I32))

        def load_scales(tile, source):
            count = 4 * source.shape[0]
            for q in range(QUADRANTS):
                nc.sync.dma_start(tile[32 * q : 32 * q + count, :].bitcast(I32), source[:, 4 * q : 4 * q + 4, :].bitcast(I32))

        def load_w1(b):
            for a in range(PASSES):
                k_rows = w1[PASS_K * a : PASS_K * (a + 1), rows(b)]
                nc.sync.dma_start(w1_raw[b][a][:], k_rows.rearrange("(p t) c -> p t c", t=4))

        def load_rows(tiles, source, b):
            nc.sync.dma_start(tiles[b][:], source[rows(b), :])

        nc.sync.dma_start(pick_at[:], offs)
        load_table(0)
        load_table(1)
        load_scales(tab_s, tab_scales)
        load_w1(0)
        load_table(2)
        nc.sync.dma_start(vec_rows[0:BLOCKS, :], gain.rearrange("(b p) -> b p", p=P))
        nc.sync.dma_start(vec_rows[BLOCKS : 2 * BLOCKS, :], knee.rearrange("(b p) -> b p", p=P))
        nc.sync.dma_start(patch_at[:], offs2)
        nc.sync.dma_start(wgs_t[:, HALVES[0]], wgs[:, HALVES[0]])
        load_rows(base_t, base, 0)
        load_rows(pg0, page0, 0)
        load_w1(1)
        nc.sync.dma_start(wgs_t[:, HALVES[1]], wgs[:, HALVES[1]])
        load_rows(base_t, base, 1)
        load_w1(2)
        nc.sync.dma_start(recall_at[:], offs3)
        load_rows(pg0, page0, 1)
        load_w1(3)
        nc.sync.dma_start(w4_w[:].bitcast(I32), w4_words[0].bitcast(I32))
        load_scales(w4_s, w4_scales)
        nc.sync.dma_start(pulse_at[:], offs4)
        nc.sync.dma_start(wgo_t[:], wgo)
        load_rows(base_t, base, 2)
        load_rows(base_t, base, 3)
        load_rows(pg0, page0, 2)
        load_rows(pg1, page1, 0)
        load_rows(pg1, page1, 1)
        load_rows(pg0, page0, 3)
        load_rows(pg1, page1, 3)
        load_rows(pg1, page1, 2)

        def pick(a, cols):
            nc.vector.tensor_copy(v_w[a][:, cols], tab_w[a][:].bitcast(U32).indirect(entries(pick_at, cols)))

        def quantise_w1(b):
            for a in range(PASSES):
                nc.scalar.copy(
                    w1_bf[b][:, PASS_K * a : PASS_K * (a + 1)].rearrange("p (c j t) -> p c t j", j=4, t=4),
                    w1_raw[b][a][:].rearrange("p t (c j) -> p c t j", j=4),
                )
            for c0, c1 in ((0, 2 * P), (2 * P, 3 * P)):
                nc.vector.quantize_mx(w1_w[b][:, c0:c1].bitcast(FP8X4), w1_s[b][:, c0:c1], w1_bf[b][:, 4 * c0 : 4 * c1])

        def add_product(b):
            for h, cols in enumerate(HALVES):
                sums = bank[2 * (b % 2) + h][:]
                for a in range(PASSES):
                    nc.tensor.matmul_mx(
                        sums,
                        lhsT=w1_w[b][:, rows(a)].bitcast(FP8X4),
                        lhsT_scale=w1_s[b][:, rows(a)],
                        rhs=v_w[a][:, cols].bitcast(FP8X4),
                        rhs_scale=v_s[4 * a : P, cols],
                        start=(a == 0),
                        stop=(a == PASSES - 1),
                    )
                nc.vector.tensor_tensor(state[b][:, cols], sums, base_t[b][:, cols], ADD)

        def make_weight(b, cols):
            nc.scalar.activation(weight[b][:, cols], wgs_t[:, cols], ACT.Copy, scale=vec_cols[:, b : b + 1])

        def patch(b):
            add_product(b)
            for cols in HALVES:
                nc.gpsimd.tensor_tensor(state[b][:, cols], state[b][:, cols], weight[b][:, cols], MULT)
            nc.vector.tensor_copy(pg0[b][:].indirect(patch_at[:]), state[b][:])

        def recall(b, cols, xr):
            nc.vector.tensor_copy(xr, pg0[b][:].indirect(entries(recall_at, cols)))

        def x_of(g, b, count=1):
            return x[g][:, WIDTHS[g] * b : WIDTHS[g] * (b + count)]

        def damp(g, b, xr, recip, sgn, via):
            knee_b = vec_cols[:, BLOCKS + b : BLOCKS + b + 1]
            nc.scalar.activation(recip, xr, ACT.Abs)
            nc.scalar.activation(sgn, recip, ACT.Sign, bias=1.0, scale=knee_b)
            nc.scalar.activation(recip, recip, ACT.Abs_reciprocal_sqrt, bias=1.0, scale=knee_b)
            nc.scalar.activation(recip, recip, ACT.Square)
            nc.gpsimd.tensor_tensor(xr, xr, sgn, MULT)
            nc.gpsimd.tensor_tensor(x_of(g, b), xr, recip, MULT)
            for j in range(WIDTHS[g] // P):
                nc.tensor.transpose(via[:, rows(j)], x_of(g, b)[:, rows(j)], ident[:])
            nc.scalar.copy(
                x_turned[g][:].rearrange("p (j u q e) -> p j u q e", u=2, q=P, e=2)[:, :, :, 32 * b : 32 * (b + 1), :],
                via[:, : WIDTHS[g]].rearrange("p (j q u e) -> p j u q e", q=32, u=2, e=2),
            )

        def quantise_x(g, banks, copy):
            pairs = x_turned[g][:].bitcast(F32)
            woven = x_woven[g][:].bitcast(F32)
            for i, via in enumerate(banks):
                piece = slice(BANK * i, BANK * (i + 1))
                for j in range(BANK // P):
                    nc.tensor.transpose(via[:, rows(j)], pairs[:, piece][:, rows(j)], ident[:])
                copy(
                    woven[:, piece].rearrange("p (j m u) -> p j m u", j=2, u=2),
                    via[:].rearrange("p (j u m) -> p j m u", j=2, u=2),
                )
            nc.vector.quantize_mx(x_w[g][:].bitcast(FP8X4), x_s[g][:], x_woven[g][:])

        def weigh(g, b, count):
            blocks = x_of(g, b, count).rearrange("p (n c) -> p n c", n=count)
            nc.gpsimd.tensor_tensor(blocks, blocks, wgo_t[:, GROUPS[g]].unsqueeze(1).to_broadcast([P, count, WIDTHS[g]]), MULT)

        def second_product(g, sums):
            for n in range(BLOCKS):
                nc.tensor.matmul_mx(
                    sums[n],
                    lhsT=w4_w[:, 2 * P * n : 2 * P * (n + 1)].bitcast(FP4X4),
                    lhsT_scale=w4_s[:, rows(n)],
                    rhs=x_w[g][:].bitcast(FP8X4),
                    rhs_scale=x_s[g][:],
                    start=True,
                    stop=True,
                )

        def scatter_pulse(g, n, values):
            nc.vector.tensor_copy(pg1[n][:].indirect(entries(pulse_at, GROUPS[g])), values)

        def pulse(g, n, sums, values):
            nc.vector.tensor_tensor(values, sums, x_of(g, n), MULT)
            scatter_pulse(g, n, values)

        pick(0, WHOLE)
        pick(1, WHOLE)
        nc.vector.tensor_copy(v_s[:], tab_s[:].indirect(pick_at[:]))
        quantise_w1(0)
        for cols in HALVES:
            pick(2, cols)
        nc.tensor.transpose(bank[4][:, :P], vec_rows[:], ident[:])
        nc.scalar.copy(vec_cols[:], bank[4][:, : 2 * BLOCKS])

        add_product(0)
        quantise_w1(1)
        for cols in HALVES:
            make_weight(0, cols)
            nc.vector.tensor_tensor(pg0[0][:].indirect(entries(patch_at, cols)), state[0][:, cols], weight[0][:, cols], MULT)
        for b in range(1, BLOCKS):
            make_weight(b, WHOLE)
        quantise_w1(2)
        quantise_w1(3)
        for b in range(1, BLOCKS):
            patch(b)

        early_recip = shared.tile([P, S + 2 * NARROW], F32, name="early_recip", offset=EARLY_RECIP_AT)
        recall(0, WHOLE, xr0[:])
        recall(1, HALVES[0], base2[:, HALVES[0]])
        for g, b in ((0, 0), (0, 1), (1, 0), (1, 1), (2, 0)):
            cols = slice(S * b + GROUPS[g].start, S * b + GROUPS[g].stop)
            damp(g, b, (xr0, base2)[b][:, GROUPS[g]], early_recip[:, cols], sign[:, cols], bank[4 + b])
        xr2_first = shared.tile([P, NARROW], F32, name="xr2_first", offset=XR2_FIRST_AT)
        recall(2, GROUPS[0], xr2_first[:])
        damp(0, 2, xr2_first[:], state[0][:, :NARROW], sign[:, 2 * S - 2 * NARROW : 2 * S - NARROW], bank[4])
        weigh(0, 0, 3)

        xr3_first = shared.tile([P, NARROW], F32, name="xr3_first", offset=XR3_FIRST_AT)
        recip3_first = shared.tile([P, NARROW], F32, name="recip3_first", offset=RECIP3_FIRST_AT)
        recall(3, GROUPS[0], xr3_first[:])
        damp(0, 3, xr3_first[:], recip3_first[:], sign[:, 2 * S - NARROW :], bank[5])
        weigh(0, 3, 1)
        quantise_x(0, [bank[6]], nc.vector.tensor_copy)

        late_width = 2 * WIDTHS[1] + 3 * WIDTHS[2]
        xr_late = shared.tile([P, late_width], F32, name="xr_late", offset=XR_LATE_AT)
        late_recip = shared.tile([P, late_width], F32, name="late_recip", offset=LATE_RECIP_AT)

        def damp_late(g, banks):
            for i, via in enumerate(banks):
                b = BLOCKS - len(banks) + i
                start = 2 * sum(WIDTHS[1:g]) + i * WIDTHS[g]
                cols = slice(start, start + WIDTHS[g])
                recall(b, GROUPS[g], xr_late[:, cols])
                damp(g, b, xr_late[:, cols], late_recip[:, cols], sign[:, cols], via)

        sums0 = [bank[n][:, :NARROW] for n in range(BLOCKS)]
        second_product(0, sums0)
        for n in (0, 1, 3):
            pulse(0, n, sums0[n], x_of(0, n))
        damp_late(1, (bank[4], bank[0]))
        quantise_x(1, [bank[7]], nc.scalar.copy)
        held = shared.tile([P, NARROW], F32, name="held", offset=X_WOVEN_AT + 8 * GROUPS[1].start)
        pulse(0, 2, sums0[2], held[:])

        sums1 = [bank[n][:, NARROW:] for n in range(BLOCKS)]
        second_product(1, sums1)
        for n in range(BLOCKS):
            if n % 2 == 0:
                weigh(1, n, 2)
            pulse(1, n, sums1[n], x_of(1, n))
        damp_late(2, (bank[5], bank[4], bank[5]))
        quantise_x(2, [bank[6], bank[7]], nc.scalar.copy)

        weigh(2, 0, BLOCKS)
        sums2 = [bank[i][:] for i in (0, 1, 4, 5)]
        second_product(2, sums2)
        for n in range(BLOCKS):
            if n == 0:
                pulse(2, n, sums2[n], x_of(2, n))
            else:
                staged = state[1 + n % 2][:, GROUPS[2]]
                nc.scalar.copy(staged, sums2[n])
                nc.gpsimd.tensor_tensor(x_of(2, n), staged, x_of(2, n), MULT)
                scatter_pulse(2, n, x_of(2, n))
            nc.sync.dma_start(out[rows(n), :], pg1[n][:])
